import numpy as np
import ml_dtypes


def mxq(x, axis, fmt="e4m3"):
    dtype, down = {"e4m3": (ml_dtypes.float8_e4m3fn, 7), "e5m2": (ml_dtypes.float8_e5m2, 14)}[fmt]
    v = np.moveaxis(np.asarray(x, np.float32).astype(ml_dtypes.bfloat16).astype(np.float64), axis, -1)
    blocks = v.reshape(v.shape[:-1] + (-1, 32))
    amax = np.abs(blocks).max(-1, keepdims=True)
    byte = np.maximum(np.where(amax > 0, np.frexp(amax)[1] - 1 + 127, 0) - down, 1)
    scale = np.exp2(byte - 127.0)
    codes = (blocks / scale).astype(np.float32).astype(dtype).astype(np.float64)
    return np.moveaxis((codes * scale).reshape(v.shape), -1, axis)


WIDE = False


def mx_kscale(k):
    if not WIDE:
        return np.ones(k)
    levels = np.array([10, -10, 5, -5, 0])
    if k % 512:
        return np.exp2(np.random.permutation(np.resize(levels, k // 32))).repeat(32)
    a = np.empty((k // 512, 16))
    for p in range(k // 512):
        a[p, :8] = np.random.permutation(np.resize(levels, 8))
        for g in range(8):
            far = levels[np.abs(levels - a[p, g]) >= 10]
            a[p, g + 8] = far[np.random.randint(len(far))]
    return np.exp2(a.ravel()).repeat(32)


def f64(x):
    return np.asarray(x).astype(np.float64)


def striped(idx):
    return np.tile(idx.reshape(-1, 16).T, (8, 1)).astype(np.uint16)


def unstriped(offs):
    return offs[:16].T.reshape(-1).astype(np.int64)


def striped8(idx):
    return np.concatenate([x.reshape(-1, 16).T for x in idx]).astype(np.uint16)


def runs(offs, k):
    lists = np.stack([offs[16 * r : 16 * r + 16].T.reshape(-1) for r in range(8)]).astype(np.int64)
    return lists[np.arange(k) % 512 // 64]


def pack_weight(w):
    k, n = w.shape
    w = f64(np.asarray(w, np.float32).astype(ml_dtypes.bfloat16)).reshape(k // 32, 32, n)
    amax = np.abs(w).max(1)
    byte = np.clip(np.where(amax > 0, np.frexp(amax)[1] - 1 + 127 - 7, 1), 1, 254)
    scaled = (w * np.exp2(127.0 - byte)[:, None, :]).reshape(k, n).astype(np.float32)
    words = np.ascontiguousarray(scaled.reshape(k // 512, 128, 4, n).transpose(0, 1, 3, 2)).astype(ml_dtypes.float8_e4m3fn).view(np.uint8)
    return words, np.ascontiguousarray(byte.astype(np.uint8).reshape(k // 512, 16, n))


def unpack_weight(words, scales):
    g, p, n, _ = words.shape
    vals = np.ascontiguousarray(words).view(ml_dtypes.float8_e4m3fn).astype(np.float64) * np.repeat(np.exp2(scales.astype(np.float64) - 127.0), 8, axis=1)[..., None]
    return vals.transpose(0, 1, 3, 2).reshape(g * 512, n)


E2M1 = np.array([0.0, 0.5, 1.0, 1.5, 2.0, 3.0, 4.0, 6.0, -0.0, -0.5, -1.0, -1.5, -2.0, -3.0, -4.0, -6.0])


def pack_fp4(w):
    k, n = w.shape
    w = f64(np.asarray(w, np.float32).astype(ml_dtypes.bfloat16)).reshape(k // 32, 32, n)
    amax = np.abs(w).max(1)
    mant, ex = np.frexp(amax / 6.0)
    byte = np.clip(np.where(amax > 0, np.where(mant > 0.5, ex, ex - 1) + 127, 1), 1, 254)
    scaled = (w * np.exp2(127.0 - byte)[:, None, :]).reshape(k, n).astype(np.float32)
    c = np.ascontiguousarray(scaled.reshape(k // 512, 128, 4, n).transpose(0, 1, 3, 2)).astype(ml_dtypes.float4_e2m1fn).view(np.uint8) & 0xF
    words = (c[..., 0::2] | (c[..., 1::2] << 4)).reshape(k // 512, 128, 2 * n)
    return np.ascontiguousarray(words), np.ascontiguousarray(byte.astype(np.uint8).reshape(k // 512, 16, n))


def unpack_fp4(words, scales):
    g, _, n = scales.shape
    words = np.ascontiguousarray(words).reshape(g, 128, n, 2)
    nib = np.empty((g, 128, n, 4), np.uint8)
    nib[..., 0::2] = words & 0xF
    nib[..., 1::2] = words >> 4
    vals = E2M1[nib] * np.repeat(np.exp2(scales.astype(np.float64) - 127.0), 8, axis=1)[..., None]
    return vals.transpose(0, 1, 3, 2).reshape(g * 512, n)


def sigmoid(v):
    return 1.0 / (1.0 + np.exp(-np.maximum(v, -700.0)))

def planes(y):
    n, m = y.shape
    v = y.astype(np.float32).astype(ml_dtypes.bfloat16).astype(np.float64).reshape(n // 32, 32, m)
    top = np.abs(v).max(1)
    byte = np.clip(np.where(top > 0, np.frexp(top)[1] - 1 + 127 - 7, 1), 1, 254)
    codes = (v * np.exp2(127.0 - byte)[:, None, :]).reshape(n, m).astype(np.float32).astype(ml_dtypes.float8_e4m3fn).view(np.uint8)
    words = codes.reshape(n // 512, 128, 4, m).transpose(0, 1, 3, 2)
    return np.ascontiguousarray(words), np.ascontiguousarray(byte.astype(np.uint8).reshape(n // 512, 16, m))


K, T, S, N, H, G, W, U = 512, 1024, 512, 512, 512, 2048, 256, 1024


def setup_inputs():
    n = np.random.standard_normal
    s = mx_kscale(K)[:, None]
    u = mx_kscale(S)
    packed_xT = pack_weight(n((K, T)) * s)
    packed_w1 = pack_fp4(n((K, H)) / np.sqrt(K) / s)
    packed_dT = pack_weight(n((K, G)) / s)
    packed_w2 = pack_fp4(n((H, N)) / np.sqrt(2 * H) / u[:, None])
    packed_w3 = pack_fp4(n((H, N)) / np.sqrt(2 * H) / u[:, None])
    perm = np.random.permutation(S)
    return {
        "x_words": packed_xT[0],
        "x_scales": packed_xT[1],
        "w1_words": packed_w1[0],
        "w1_scales": packed_w1[1],
        "d_words": packed_dT[0],
        "d_scales": packed_dT[1],
        "gn": (np.random.uniform(0.5, 1.5, (H, 1)) * u[:, None]).astype(np.float32),
        "gk": (np.random.uniform(0.5, 1.5, (H, 1)) * u[:, None]).astype(np.float32),
        "w2_words": packed_w2[0],
        "w2_scales": packed_w2[1],
        "w3_words": packed_w3[0],
        "w3_scales": packed_w3[1],
        "offs": striped(np.random.permutation(T)[:S]),
        "kidx": striped8(np.random.randint(0, G, (8, H))),
        "two": striped(np.random.permutation(T)[:S]),
        "n1": striped(perm[:W]),
        "n2": striped(perm[W:]),
        "n3": striped(np.random.randint(0, S, U)),
        "n4": striped(np.random.permutation(S)),
        "n5": striped(np.random.permutation(S)),
        "n6": striped(np.random.permutation(S)),
    }


def reference(x_words, x_scales, w1_words, w1_scales, d_words, d_scales, gn, gk, w2_words, w2_scales, w3_words, w3_scales, offs, kidx, two, n1, n2, n3, n4, n5, n6):
    xq = unpack_weight(x_words, x_scales)[:, unstriped(offs)]
    y = unpack_fp4(w1_words, w1_scales).T @ xq
    pa = y[:, unstriped(n1)]
    pb = y[:, unstriped(n2)]
    rb = np.maximum(0.5 * pa, pb)
    ra = pb - pa
    ds = np.zeros((H, S))
    ds[:, unstriped(n1)] = ra
    dt = ds.copy()
    dt[:, unstriped(n2)] = rb
    z = f64(gn) * dt
    d_kidx = unpack_weight(d_words, d_scales)[np.arange(K)[:, None], runs(kidx, K)]
    x_two = unpack_weight(x_words, x_scales)[:, unstriped(two)]
    s = 0.0625 * (d_kidx.T @ x_two)
    mb = s[:, unstriped(n3)]
    mx = mb.reshape(H, S, 2).max(axis=2)
    st = s - mx
    z2 = f64(gk) * (np.maximum(st, st[:, unstriped(n4)]))
    h = unpack_fp4(w2_words, w2_scales).T @ mxq(z, 0, "e4m3") + unpack_fp4(w3_words, w3_scales).T @ mxq(z2, 0, "e4m3")
    st2 = h * (sigmoid(h[:, unstriped(n5)]))
    out_0 = st2 - st2[:, unstriped(n6)]
    return (out_0,) + planes(out_0)

@@ -1,0 +1,307 @@
+from contextlib import ExitStack
+
+import concourse.mybir as mybir
+
+F32 = mybir.dt.float32
+BF16 = mybir.dt.bfloat16
+I32 = mybir.dt.int32
+U32 = mybir.dt.uint32
+U16 = mybir.dt.uint16
+U8 = mybir.dt.uint8
+FP8X4 = mybir.dt.float8_e4m3fn_x4
+FP4X4 = mybir.dt.float4_e2m1fn_x4
+ALU = mybir.AluOpType
+COPY = mybir.ActivationFunctionType.Copy
+SIGMOID = mybir.ActivationFunctionType.Sigmoid
+
+P = 128
+PACK = 4
+COLS = 512
+TOKENS = 1024
+CODEWORDS = 2048
+HALF = COLS // 2
+LIST_ROWS = 16
+QUADS = 4
+SPARE = 16
+Y_ON_VECTOR = (1,)
+
+FLOPS = 4 * 2 * 512 * 512 * 512
+
+
+def tile_picked_jkeyliftghopmhopg_none_po_kernel(
+    tc, x_words, x_scales, w1_words, w1_scales, d_words, d_scales, gn, gk, w2_words, w2_scales,
+    w3_words, w3_scales, offs, kidx, two, n1, n2, n3, n4, n5, n6, out_0, out_1, out_2,
+):
+    nc = tc.nc
+
+    with ExitStack() as ctx:
+        keep = ctx.enter_context(tc.tile_pool(name="keep", bufs=1))
+        psum = ctx.enter_context(tc.psum_pool(name="psum", bufs=1))
+
+        def new(name, shape, dtype, tag=None):
+            return keep.tile(shape, dtype, name=name, tag=tag or name, align_bytes=64)
+
+        def load_list(name, src):
+            lst = new(name, list(src.shape), U16)
+            nc.sync.dma_start(lst[:], src)
+            return lst
+
+        def entries(lst, start, count):
+            return lst[:, start // LIST_ROWS : (start + count) // LIST_ROWS]
+
+        def zeroed_bytes(name, width, engine):
+            plane = new(name, [P, width], U8)
+            engine.memset(plane[:].bitcast(I32), 0)
+            return plane
+
+        def load_scale_rows(plane, scales):
+            for q in range(QUADS):
+                nc.sync.dma_start(plane[32 * q : 32 * q + 4, :].bitcast(I32), scales[0, 4 * q : 4 * q + 4, :].bitcast(I32))
+
+        def load_fp4_words(name, words):
+            raw = new(name, [P, 2 * COLS], U8)
+            nc.sync.dma_start(raw[:].bitcast(I32), words[0].bitcast(I32))
+            return raw
+
+        def deal_fp4(codes, scales, raw_codes, raw_scales, tiles, engine):
+            engine.tensor_copy(
+                codes[:].rearrange("p (t m b) -> p t m b", t=PACK, b=2)[:, tiles],
+                raw_codes[:].rearrange("p (m t b) -> p t m b", t=PACK, b=2)[:, tiles],
+            )
+            engine.tensor_copy(
+                scales[:].rearrange("p (t m) -> p t m", t=PACK)[:, tiles],
+                raw_scales[:].rearrange("p (m t) -> p t m", t=PACK)[:, tiles],
+            )
+
+        def deal_columns(name, raw, dtype, engine):
+            dealt = new(name, [P, COLS], dtype)
+            engine.tensor_copy(
+                dealt[:].rearrange("p (t m) -> p t m", t=PACK),
+                raw.rearrange("p (m t) -> p t m", t=PACK),
+            )
+            return dealt
+
+        def gather_codes(name, table, lst, dtype):
+            picked = new(name, [P, COLS], dtype)
+            nc.vector.tensor_copy(picked[:], table.indirect(lst[:]))
+            return picked
+
+        x_scale_table = zeroed_bytes("x_scale_table", TOKENS, nc.gpsimd)
+        w1_scale_raw = zeroed_bytes("w1_scale_raw", COLS, nc.gpsimd)
+        d_scale_table = zeroed_bytes("d_scale_table", CODEWORDS, nc.gpsimd)
+        key_scales = zeroed_bytes("key_scales", COLS, nc.gpsimd)
+        w2_scale_raw = zeroed_bytes("w2_scale_raw", COLS, nc.gpsimd)
+        w3_scale_raw = zeroed_bytes("w3_scale_raw", COLS, nc.gpsimd)
+
+        offs_l = load_list("offs_l", offs)
+        load_scale_rows(x_scale_table, x_scales)
+        x_table = new("x_table", [P, TOKENS], U32)
+        nc.sync.dma_start(x_table[:].bitcast(I32), x_words[0].rearrange("p n t -> p (n t)").bitcast(I32))
+        w1_raw = load_fp4_words("w1_raw", w1_words)
+        load_scale_rows(w1_scale_raw, w1_scales)
+        kidx_l = load_list("kidx_l", kidx)
+        for e in range(2):
+            nc.sync.dma_start(d_scale_table[e:P:LIST_ROWS, :].bitcast(I32), d_scales[0, e:16:2, :].bitcast(I32))
+        n1_l = load_list("n1_l", n1)
+        n2_l = load_list("n2_l", n2)
+        d_table = new("d_table", [P, CODEWORDS], U32)
+        nc.sync.dma_start(d_table[:].bitcast(I32), d_words[0].rearrange("p n t -> p (n t)").bitcast(I32))
+        two_l = load_list("two_l", two)
+        w3_raw = load_fp4_words("w3_raw", w3_words)
+        load_scale_rows(w3_scale_raw, w3_scales)
+        w2_raw = load_fp4_words("w2_raw", w2_words)
+        load_scale_rows(w2_scale_raw, w2_scales)
+
+        w1_codes = new("w1_codes", [P, 2 * COLS], U8)
+        w1_sc = new("w1_sc", [P, COLS], U8)
+        xa_scales = gather_codes("xa_scales", x_scale_table[:], offs_l, U8)
+        xa_codes = gather_codes("xa_codes", x_table[:], offs_l, U32)
+        deal_fp4(w1_codes, w1_sc, w1_raw, w1_scale_raw, slice(0, 1), nc.vector)
+        deal_fp4(w1_codes, w1_sc, w1_raw, w1_scale_raw, slice(1, PACK), nc.vector)
+
+        def fp4_product(acc, codes, scales, t, moving, moving_scales, start, stop):
+            nc.tensor.matmul_mx(
+                acc[:],
+                lhsT=codes[:, 2 * P * t : 2 * P * (t + 1)].bitcast(FP4X4),
+                lhsT_scale=scales[:, P * t : P * (t + 1)],
+                rhs=moving[:].bitcast(FP8X4),
+                rhs_scale=moving_scales[:],
+                start=start,
+                stop=stop,
+            )
+
+        y_acc = []
+        for t in range(PACK):
+            acc = psum.tile([P, COLS], F32, name=f"y_acc{t}", tag=f"bank_a{t}")
+            fp4_product(acc, w1_codes, w1_sc, t, xa_codes, xa_scales, True, True)
+            y_acc.append(acc)
+
+        pa = new("pa", [P, PACK, HALF], F32)
+        pb = new("pb", [P, PACK, HALF], F32)
+        ra = new("ra", [P, PACK, HALF], F32)
+        rb = new("rb", [P, PACK, HALF], F32)
+
+        def pair_formulas(tiles):
+            nc.vector.tensor_tensor(ra[:, tiles, :], pb[:, tiles, :], pa[:, tiles, :], ALU.subtract)
+            nc.vector.scalar_tensor_tensor(rb[:, tiles, :], pa[:, tiles, :], 0.5, pb[:, tiles, :], ALU.mult, ALU.max)
+
+        for t in range(PACK):
+            y_t = new(f"y{t}", [P, COLS], F32)
+            if t in Y_ON_VECTOR:
+                nc.vector.tensor_copy(y_t[:], y_acc[t][:])
+            else:
+                nc.scalar.activation(y_t[:], y_acc[t][:], COPY)
+            nc.scalar.activation(pa[:, t, :], y_t[:].indirect(n1_l[:]), COPY)
+            nc.scalar.activation(pb[:, t, :], y_t[:].indirect(n2_l[:]), COPY)
+            if t == 0:
+                pair_formulas(slice(0, 1))
+
+        key_scales_picked = gather_codes("key_scales_picked", d_scale_table[:], kidx_l, U8)
+        key_scales_dealt = deal_columns("key_scales_dealt", key_scales_picked[:], U8, nc.vector)
+        for r in range(4):
+            src_row = LIST_ROWS * (r // 2) + r % 2
+            nc.sync.dma_start(key_scales[r:P:32, :].bitcast(I32), key_scales_dealt[src_row:P:32, :].bitcast(I32))
+        key_picked = gather_codes("key_picked", d_table[:], kidx_l, U32)
+        key_codes = deal_columns("key_codes", key_picked[:].bitcast(I32), I32, nc.vector)
+        xb_scales = gather_codes("xb_scales", x_scale_table[:], two_l, U8)
+        xb_codes = gather_codes("xb_codes", x_table[:], two_l, U32)
+
+        n3_l = load_list("n3_l", n3)
+        n4_l = load_list("n4_l", n4)
+        gn_t = new("gn_t", [P, PACK], F32)
+        nc.sync.dma_start(gn_t[:], gn.rearrange("(p t) o -> p (t o)", t=PACK))
+        gk_t = new("gk_t", [P, PACK], F32)
+        nc.sync.dma_start(gk_t[:], gk.rearrange("(p t) o -> p (t o)", t=PACK))
+        n5_l = load_list("n5_l", n5)
+        n6_l = load_list("n6_l", n6)
+
+        s_acc = []
+        for t in range(PACK):
+            acc = psum.tile([P, COLS], F32, name=f"s_acc{t}", tag=f"bank_b{t}")
+            nc.tensor.matmul_mx(
+                acc[:],
+                lhsT=key_codes[:, P * t : P * (t + 1)].bitcast(FP8X4),
+                lhsT_scale=key_scales[:, P * t : P * (t + 1)],
+                rhs=xb_codes[:].bitcast(FP8X4),
+                rhs_scale=xb_scales[:],
+                start=True,
+                stop=True,
+            )
+            s_acc.append(acc)
+
+        s = []
+        for t in range(PACK):
+            s_t = new(f"s{t}", [P, COLS + SPARE], F32, tag=f"window{t}")
+            nc.gpsimd.memset(s_t[:, COLS:], 0.0)
+            nc.vector.tensor_scalar(s_t[:, :COLS], s_acc[t][:], 0.0625, None, ALU.mult)
+            s.append(s_t)
+
+        pair_formulas(slice(1, PACK))
+
+        def quantise(name, pairs):
+            grouped = new(name + "_grouped", [P, COLS, PACK], BF16)
+            nc.vector.tensor_copy(
+                grouped[:].rearrange("p c t -> p (c t)").bitcast(I32).rearrange("p (c u) -> p c u", u=2),
+                pairs[:].rearrange("p u c e -> p u (c e)").bitcast(I32).rearrange("p u c -> p c u"),
+            )
+            codes = new(name + "_codes", [P, COLS], U32)
+            scales = new(name + "_scales", [P, COLS], U8)
+            nc.vector.quantize_mx(codes[:].bitcast(FP8X4), scales[:], grouped[:].rearrange("p c t -> p (c t)"))
+            return codes, scales
+
+        z2_pairs = new("z2_pairs", [P, 2, COLS, 2], BF16, tag="pairs")
+        for t in range(PACK):
+            s_t = s[t]
+            mb = new(f"mb{t}", [P, 2 * COLS], F32)
+            for i in range(2):
+                nc.scalar.activation(mb[:, i * COLS : (i + 1) * COLS], s_t[:].indirect(entries(n3_l, i * COLS, COLS)), COPY)
+            mx = new(f"mx{t}", [P, COLS], F32, tag="mx")
+            nc.vector.tensor_tensor(mx[:], mb[:, 0 : 2 * COLS : 2], mb[:, 1 : 2 * COLS : 2], ALU.max)
+            st = new(f"st{t}", [P, COLS], F32)
+            nc.vector.scalar_tensor_tensor(st[:], s_acc[t][:], 0.0625, mx[:], ALU.mult, ALU.subtract)
+            st_n4 = new(f"st_n4_{t}", [P, COLS], F32)
+            for i in range(2):
+                nc.vector.tensor_copy(st_n4[:, i * HALF : (i + 1) * HALF], st[:].indirect(entries(n4_l, i * HALF, HALF)))
+            larger = new(f"larger{t}", [P, COLS], F32)
+            nc.vector.tensor_tensor(larger[:], st[:], st_n4[:], ALU.max)
+            nc.vector.tensor_scalar(z2_pairs[:, t // 2, :, t % 2], larger[:], gk_t[:, t : t + 1], None, ALU.mult)
+
+        w3_codes = new("w3_codes", [P, 2 * COLS], U8)
+        w3_sc = new("w3_sc", [P, COLS], U8)
+        deal_fp4(w3_codes, w3_sc, w3_raw, w3_scale_raw, slice(0, PACK), nc.gpsimd)
+        w2_codes = new("w2_codes", [P, 2 * COLS], U8)
+        w2_sc = new("w2_sc", [P, COLS], U8)
+        deal_fp4(w2_codes, w2_sc, w2_raw, w2_scale_raw, slice(0, PACK), nc.gpsimd)
+        z2_codes, z2_scales = quantise("z2", z2_pairs)
+
+        z_pairs = new("z_pairs", [P, 2, COLS, 2], BF16, tag="pairs")
+        for t in range(PACK):
+            dt = new(f"dt{t}", [P, COLS], F32, tag=f"window{t}" if t > 0 else None)
+            nc.scalar.activation(dt[:].indirect(n1_l[:]), ra[:, t, :], COPY)
+            nc.scalar.activation(dt[:].indirect(n2_l[:]), rb[:, t, :], COPY)
+            nc.vector.tensor_scalar(z_pairs[:, t // 2, :, t % 2], dt[:], gn_t[:, t : t + 1], None, ALU.mult)
+        z_codes, z_scales = quantise("z", z_pairs)
+
+        h_acc = []
+        for t in range(PACK):
+            acc = psum.tile([P, COLS], F32, name=f"h_acc{t}", tag=f"bank_a{t}")
+            fp4_product(acc, w3_codes, w3_sc, t, z2_codes, z2_scales, True, False)
+            h_acc.append(acc)
+        for t in range(PACK):
+            fp4_product(h_acc[t], w2_codes, w2_sc, t, z_codes, z_scales, False, True)
+
+        result = new("result", [P, PACK, COLS], F32)
+        rounded = new("rounded", [P, COLS, PACK], BF16)
+        out_rows = out_0.rearrange("(p t) c -> p t c", t=PACK)
+        h, st2, st2_n6 = [], [], []
+        for t in range(PACK):
+            h_t = new(f"h{t}", [P, COLS], F32)
+            nc.vector.tensor_copy(h_t[:], h_acc[t][:])
+            h.append(h_t)
+        out_codes = new("out_codes", [P, COLS], U32)
+        out_scales = new("out_scales", [P, COLS], U8)
+        out_words = out_1[0].rearrange("p n t -> p (n t)").bitcast(I32)
+
+        def subtract(t, cols):
+            nc.vector.tensor_tensor(result[:, t, cols], st2[t][:, cols], st2_n6[t][:, cols], ALU.subtract)
+            nc.sync.dma_start(out_rows[:, t, cols], result[:, t, cols])
+
+        def round_pair(t, cols):
+            nc.vector.tensor_copy(rounded[:, cols, t : t + 2], result[:, t : t + 2, cols].rearrange("p e c -> p c e"))
+
+        whole = slice(0, COLS)
+
+        def fetch_n6(t):
+            fetched = new(f"st2_n6_{t}", [P, COLS], F32)
+            for i in range(2):
+                cols = slice(i * HALF, (i + 1) * HALF)
+                looked_up = st2[t][:].indirect(entries(n6_l, i * HALF, HALF))
+                if t == 0:
+                    nc.vector.tensor_copy(fetched[:, cols], looked_up)
+                else:
+                    nc.scalar.activation(fetched[:, cols], looked_up, COPY)
+            st2_n6.append(fetched)
+
+        for t in range(PACK):
+            gate = new(f"gate{t}", [P, COLS], F32)
+            for i in range(2):
+                nc.scalar.activation(gate[:, i * HALF : (i + 1) * HALF], h[t][:].indirect(entries(n5_l, i * HALF, HALF)), SIGMOID)
+            st2_t = new(f"st2_{t}", [P, COLS], F32)
+            nc.vector.tensor_tensor(st2_t[:], h[t][:], gate[:], ALU.mult)
+            st2.append(st2_t)
+            if t == 0:
+                fetch_n6(0)
+                subtract(0, whole)
+        for t in range(1, PACK):
+            fetch_n6(t)
+        subtract(1, whole)
+        round_pair(0, whole)
+        subtract(2, whole)
+        for i in range(2):
+            cols = slice(i * HALF, (i + 1) * HALF)
+            subtract(3, cols)
+            round_pair(2, cols)
+            nc.vector.quantize_mx(out_codes[:, cols].bitcast(FP8X4), out_scales[:, cols], rounded[:, cols, :].rearrange("p c t -> p (c t)"))
+            nc.sync.dma_start(out_words[:, cols], out_codes[:, cols].bitcast(I32))
+        for q in range(QUADS):
+            nc.sync.dma_start(out_2[0, 4 * q : 4 * q + 4, :].bitcast(I32), out_scales[32 * q : 32 * q + 4, :].bitcast(I32))

@@ -63,19 +63,18 @@ def tile_picked_jkeyliftghopmhopg_none_po_kernel(
             nc.sync.dma_start(raw[:].bitcast(I32), words[0].bitcast(I32))
             return raw
 
-        def deal_fp4(codes, scales, raw_codes, raw_scales, tiles, engine):
-            engine.tensor_copy(
-                codes[:].rearrange("p (t m b) -> p t m b", t=PACK, b=2)[:, tiles],
-                raw_codes[:].rearrange("p (m t b) -> p t m b", t=PACK, b=2)[:, tiles],
+        def deal_fp4_words(name, raw, tiles, tag=None):
+            count = tiles.stop - tiles.start
+            dealt = new(name, [P, 2 * P * count], U8, tag=tag)
+            nc.vector.tensor_copy(
+                dealt[:].rearrange("p (t m b) -> p t m b", t=count, b=2),
+                raw[:].rearrange("p (m t b) -> p t m b", t=PACK, b=2)[:, tiles],
             )
-            engine.tensor_copy(
-                scales[:].rearrange("p (t m) -> p t m", t=PACK)[:, tiles],
-                raw_scales[:].rearrange("p (m t) -> p t m", t=PACK)[:, tiles],
-            )
+            return [dealt[:, 2 * P * i : 2 * P * (i + 1)] for i in range(count)]
 
-        def deal_columns(name, raw, dtype, engine):
-            dealt = new(name, [P, COLS], dtype)
-            engine.tensor_copy(
+        def deal_columns(name, raw, dtype, tag=None):
+            dealt = new(name, [P, COLS], dtype, tag=tag)
+            nc.vector.tensor_copy(
                 dealt[:].rearrange("p (t m) -> p t m", t=PACK),
                 raw.rearrange("p (m t) -> p t m", t=PACK),
             )
@@ -104,28 +103,24 @@ def tile_picked_jkeyliftghopmhopg_none_po_kernel(
             nc.sync.dma_start(d_scale_table[e:P:LIST_ROWS, :].bitcast(I32), d_scales[0, e:16:2, :].bitcast(I32))
         n1_l = load_list("n1_l", n1)
         n2_l = load_list("n2_l", n2)
+        two_l = load_list("two_l", two)
         d_table = new("d_table", [P, CODEWORDS], U32)
         nc.sync.dma_start(d_table[:].bitcast(I32), d_words[0].rearrange("p n t -> p (n t)").bitcast(I32))
-        two_l = load_list("two_l", two)
-        w3_raw = load_fp4_words("w3_raw", w3_words)
-        load_scale_rows(w3_scale_raw, w3_scales)
-        w2_raw = load_fp4_words("w2_raw", w2_words)
-        load_scale_rows(w2_scale_raw, w2_scales)
+        n3_l = load_list("n3_l", n3)
 
-        w1_codes = new("w1_codes", [P, 2 * COLS], U8)
-        w1_sc = new("w1_sc", [P, COLS], U8)
         xa_scales = gather_codes("xa_scales", x_scale_table[:], offs_l, U8)
         xa_codes = gather_codes("xa_codes", x_table[:], offs_l, U32)
-        deal_fp4(w1_codes, w1_sc, w1_raw, w1_scale_raw, slice(0, 1), nc.vector)
-        deal_fp4(w1_codes, w1_sc, w1_raw, w1_scale_raw, slice(1, PACK), nc.vector)
+        w1_codes = deal_fp4_words("w1_codes_first", w1_raw, slice(0, 1))
+        w1_sc = deal_columns("w1_sc", w1_scale_raw[:], U8)
+        w1_codes = w1_codes + deal_fp4_words("w1_codes_rest", w1_raw, slice(1, PACK), tag="w1_scale_raw")
 
         def fp4_product(acc, codes, scales, t, moving, moving_scales, start, stop):
             nc.tensor.matmul_mx(
-                acc[:],
-                lhsT=codes[:, 2 * P * t : 2 * P * (t + 1)].bitcast(FP4X4),
+                acc,
+                lhsT=codes[t].bitcast(FP4X4),
                 lhsT_scale=scales[:, P * t : P * (t + 1)],
-                rhs=moving[:].bitcast(FP8X4),
-                rhs_scale=moving_scales[:],
+                rhs=moving.bitcast(FP8X4),
+                rhs_scale=moving_scales,
                 start=start,
                 stop=stop,
             )
@@ -133,17 +128,16 @@ def tile_picked_jkeyliftghopmhopg_none_po_kernel(
         y_acc = []
         for t in range(PACK):
             acc = psum.tile([P, COLS], F32, name=f"y_acc{t}", tag=f"bank_a{t}")
-            fp4_product(acc, w1_codes, w1_sc, t, xa_codes, xa_scales, True, True)
+            fp4_product(acc[:], w1_codes, w1_sc, t, xa_codes[:], xa_scales[:], True, True)
             y_acc.append(acc)
 
         pa = new("pa", [P, PACK, HALF], F32)
         pb = new("pb", [P, PACK, HALF], F32)
-        ra = new("ra", [P, PACK, HALF], F32)
-        rb = new("rb", [P, PACK, HALF], F32)
-
-        def pair_formulas(tiles):
-            nc.vector.tensor_tensor(ra[:, tiles, :], pb[:, tiles, :], pa[:, tiles, :], ALU.subtract)
-            nc.vector.scalar_tensor_tensor(rb[:, tiles, :], pa[:, tiles, :], 0.5, pb[:, tiles, :], ALU.mult, ALU.max)
+        def differences(name, tiles, tag=None):
+            count = tiles.stop - tiles.start
+            diff = new(name, [P, count, HALF], F32, tag=tag)
+            nc.vector.tensor_tensor(diff[:], pb[:, tiles, :], pa[:, tiles, :], ALU.subtract)
+            return [diff[:, i, :] for i in range(count)]
 
         for t in range(PACK):
             y_t = new(f"y{t}", [P, COLS], F32)
@@ -154,24 +148,31 @@ def tile_picked_jkeyliftghopmhopg_none_po_kernel(
             nc.scalar.activation(pa[:, t, :], y_t[:].indirect(n1_l[:]), COPY)
             nc.scalar.activation(pb[:, t, :], y_t[:].indirect(n2_l[:]), COPY)
             if t == 0:
-                pair_formulas(slice(0, 1))
+                ra = differences("ra_first", slice(0, 1))
 
         key_scales_picked = gather_codes("key_scales_picked", d_scale_table[:], kidx_l, U8)
-        key_scales_dealt = deal_columns("key_scales_dealt", key_scales_picked[:], U8, nc.vector)
+        key_scales_dealt = deal_columns("key_scales_dealt", key_scales_picked[:], U8)
         for r in range(4):
             src_row = LIST_ROWS * (r // 2) + r % 2
             nc.sync.dma_start(key_scales[r:P:32, :].bitcast(I32), key_scales_dealt[src_row:P:32, :].bitcast(I32))
-        key_picked = gather_codes("key_picked", d_table[:], kidx_l, U32)
-        key_codes = deal_columns("key_codes", key_picked[:].bitcast(I32), I32, nc.vector)
         xb_scales = gather_codes("xb_scales", x_scale_table[:], two_l, U8)
+        key_picked = gather_codes("key_picked", d_table[:], kidx_l, U32)
+        key_codes = new("key_codes", [P, COLS], I32)
+        nc.vector.tensor_copy(
+            key_codes[:].rearrange("p (t m) -> p m t", t=PACK),
+            key_picked[:].bitcast(I32).rearrange("p (m t) -> p m t", t=PACK),
+        )
         xb_codes = gather_codes("xb_codes", x_table[:], two_l, U32)
 
-        n3_l = load_list("n3_l", n3)
         n4_l = load_list("n4_l", n4)
         gn_t = new("gn_t", [P, PACK], F32)
         nc.sync.dma_start(gn_t[:], gn.rearrange("(p t) o -> p (t o)", t=PACK))
         gk_t = new("gk_t", [P, PACK], F32)
         nc.sync.dma_start(gk_t[:], gk.rearrange("(p t) o -> p (t o)", t=PACK))
+        w3_raw = load_fp4_words("w3_raw", w3_words)
+        load_scale_rows(w3_scale_raw, w3_scales)
+        w2_raw = load_fp4_words("w2_raw", w2_words)
+        load_scale_rows(w2_scale_raw, w2_scales)
         n5_l = load_list("n5_l", n5)
         n6_l = load_list("n6_l", n6)
 
@@ -196,17 +197,23 @@ def tile_picked_jkeyliftghopmhopg_none_po_kernel(
             nc.vector.tensor_scalar(s_t[:, :COLS], s_acc[t][:], 0.0625, None, ALU.mult)
             s.append(s_t)
 
-        pair_formulas(slice(1, PACK))
+        rb = new("rb", [P, PACK, HALF], F32, tag="xb_codes")
+        nc.vector.scalar_tensor_tensor(rb[:], pa[:], 0.5, pb[:], ALU.mult, ALU.max)
+        ra = ra + differences("ra_rest", slice(1, PACK), tag="key_codes")
 
-        def quantise(name, pairs):
+        whole = slice(0, COLS)
+        halves = [slice(0, HALF), slice(HALF, COLS)]
+
+        def quantise(name, pairs, spans):
             grouped = new(name + "_grouped", [P, COLS, PACK], BF16)
-            nc.vector.tensor_copy(
-                grouped[:].rearrange("p c t -> p (c t)").bitcast(I32).rearrange("p (c u) -> p c u", u=2),
-                pairs[:].rearrange("p u c e -> p u (c e)").bitcast(I32).rearrange("p u c -> p c u"),
-            )
+            grouped_words = grouped[:].rearrange("p c t -> p (c t)").bitcast(I32).rearrange("p (c u) -> p c u", u=2)
+            pair_words = pairs[:].rearrange("p u c e -> p u (c e)").bitcast(I32).rearrange("p u c -> p c u")
             codes = new(name + "_codes", [P, COLS], U32)
             scales = new(name + "_scales", [P, COLS], U8)
-            nc.vector.quantize_mx(codes[:].bitcast(FP8X4), scales[:], grouped[:].rearrange("p c t -> p (c t)"))
+            for cols in spans:
+                nc.vector.tensor_copy(grouped_words[:, cols, :], pair_words[:, cols, :])
+            for cols in spans:
+                nc.vector.quantize_mx(codes[:, cols].bitcast(FP8X4), scales[:, cols], grouped[:, cols, :].rearrange("p c t -> p (c t)"))
             return codes, scales
 
         z2_pairs = new("z2_pairs", [P, 2, COLS, 2], BF16, tag="pairs")
@@ -226,34 +233,34 @@ def tile_picked_jkeyliftghopmhopg_none_po_kernel(
             nc.vector.tensor_tensor(larger[:], st[:], st_n4[:], ALU.max)
             nc.vector.tensor_scalar(z2_pairs[:, t // 2, :, t % 2], larger[:], gk_t[:, t : t + 1], None, ALU.mult)
 
-        w3_codes = new("w3_codes", [P, 2 * COLS], U8)
-        w3_sc = new("w3_sc", [P, COLS], U8)
-        deal_fp4(w3_codes, w3_sc, w3_raw, w3_scale_raw, slice(0, PACK), nc.gpsimd)
-        w2_codes = new("w2_codes", [P, 2 * COLS], U8)
-        w2_sc = new("w2_sc", [P, COLS], U8)
-        deal_fp4(w2_codes, w2_sc, w2_raw, w2_scale_raw, slice(0, PACK), nc.gpsimd)
-        z2_codes, z2_scales = quantise("z2", z2_pairs)
+        w3_codes = deal_fp4_words("w3_codes", w3_raw, slice(0, PACK), tag="key_picked")
+        w3_sc = deal_columns("w3_sc", w3_scale_raw[:], U8, tag="xb_scales")
+        w2_codes = deal_fp4_words("w2_codes", w2_raw, slice(0, PACK), tag="mb0")
+        w2_sc = deal_columns("w2_sc", w2_scale_raw[:], U8, tag="key_scales")
+        z2_codes, z2_scales = quantise("z2", z2_pairs, [whole])
 
         z_pairs = new("z_pairs", [P, 2, COLS, 2], BF16, tag="pairs")
         for t in range(PACK):
             dt = new(f"dt{t}", [P, COLS], F32, tag=f"window{t}" if t > 0 else None)
-            nc.scalar.activation(dt[:].indirect(n1_l[:]), ra[:, t, :], COPY)
+            nc.scalar.activation(dt[:].indirect(n1_l[:]), ra[t], COPY)
             nc.scalar.activation(dt[:].indirect(n2_l[:]), rb[:, t, :], COPY)
-            nc.vector.tensor_scalar(z_pairs[:, t // 2, :, t % 2], dt[:], gn_t[:, t : t + 1], None, ALU.mult)
-        z_codes, z_scales = quantise("z", z_pairs)
+            for cols in halves if t == PACK - 1 else [whole]:
+                nc.vector.tensor_scalar(z_pairs[:, t // 2, cols, t % 2], dt[:, cols], gn_t[:, t : t + 1], None, ALU.mult)
+        z_codes, z_scales = quantise("z", z_pairs, halves)
 
         h_acc = []
         for t in range(PACK):
             acc = psum.tile([P, COLS], F32, name=f"h_acc{t}", tag=f"bank_a{t}")
-            fp4_product(acc, w3_codes, w3_sc, t, z2_codes, z2_scales, True, False)
+            fp4_product(acc[:], w3_codes, w3_sc, t, z2_codes[:], z2_scales[:], True, False)
             h_acc.append(acc)
         for t in range(PACK):
-            fp4_product(h_acc[t], w2_codes, w2_sc, t, z_codes, z_scales, False, True)
+            for cols in halves:
+                fp4_product(h_acc[t][:, cols], w2_codes, w2_sc, t, z_codes[:, cols], z_scales[:, cols], False, cols == halves[-1])
 
         result = new("result", [P, PACK, COLS], F32)
         rounded = new("rounded", [P, COLS, PACK], BF16)
         out_rows = out_0.rearrange("(p t) c -> p t c", t=PACK)
-        h, st2, st2_n6 = [], [], []
+        h, st2 = [], []
         for t in range(PACK):
             h_t = new(f"h{t}", [P, COLS], F32)
             nc.vector.tensor_copy(h_t[:], h_acc[t][:])
@@ -262,45 +269,38 @@ def tile_picked_jkeyliftghopmhopg_none_po_kernel(
         out_scales = new("out_scales", [P, COLS], U8)
         out_words = out_1[0].rearrange("p n t -> p (n t)").bitcast(I32)
 
-        def subtract(t, cols):
-            nc.vector.tensor_tensor(result[:, t, cols], st2[t][:, cols], st2_n6[t][:, cols], ALU.subtract)
+        def subtract(t, cols, fetched):
+            nc.vector.tensor_tensor(result[:, t, cols], st2[t][:, cols], fetched, ALU.subtract)
             nc.sync.dma_start(out_rows[:, t, cols], result[:, t, cols])
 
-        def round_pair(t, cols):
-            nc.vector.tensor_copy(rounded[:, cols, t : t + 2], result[:, t : t + 2, cols].rearrange("p e c -> p c e"))
-
-        whole = slice(0, COLS)
-
-        def fetch_n6(t):
-            fetched = new(f"st2_n6_{t}", [P, COLS], F32)
-            for i in range(2):
-                cols = slice(i * HALF, (i + 1) * HALF)
-                looked_up = st2[t][:].indirect(entries(n6_l, i * HALF, HALF))
-                if t == 0:
-                    nc.vector.tensor_copy(fetched[:, cols], looked_up)
-                else:
-                    nc.scalar.activation(fetched[:, cols], looked_up, COPY)
-            st2_n6.append(fetched)
+        def fetch_n6(fetched, t, i):
+            looked_up = st2[t][:].indirect(entries(n6_l, i * HALF, HALF))
+            if t == 0:
+                nc.vector.tensor_copy(fetched, looked_up)
+            else:
+                nc.scalar.activation(fetched, looked_up, COPY)
 
         for t in range(PACK):
             gate = new(f"gate{t}", [P, COLS], F32)
             for i in range(2):
-                nc.scalar.activation(gate[:, i * HALF : (i + 1) * HALF], h[t][:].indirect(entries(n5_l, i * HALF, HALF)), SIGMOID)
+                nc.scalar.activation(gate[:, halves[i]], h[t][:].indirect(entries(n5_l, i * HALF, HALF)), SIGMOID)
             st2_t = new(f"st2_{t}", [P, COLS], F32)
             nc.vector.tensor_tensor(st2_t[:], h[t][:], gate[:], ALU.mult)
             st2.append(st2_t)
             if t == 0:
-                fetch_n6(0)
-                subtract(0, whole)
-        for t in range(1, PACK):
-            fetch_n6(t)
-        subtract(1, whole)
-        round_pair(0, whole)
-        subtract(2, whole)
-        for i in range(2):
-            cols = slice(i * HALF, (i + 1) * HALF)
-            subtract(3, cols)
-            round_pair(2, cols)
+                fetched_first = new("st2_n6_first", [P, COLS], F32)
+                for i in range(2):
+                    fetch_n6(fetched_first[:, halves[i]], 0, i)
+        subtract(0, whole, fetched_first[:])
+        for i, cols in enumerate(halves):
+            fetched = new(f"st2_n6_half{i}", [P, PACK - 1, HALF], F32, tag="gate3" if i == 1 else None)
+            for t in range(1, PACK):
+                fetch_n6(fetched[:, t - 1, :], t, i)
+                subtract(t, cols, fetched[:, t - 1, :])
+            nc.vector.tensor_copy(
+                rounded[:, cols, :].rearrange("p (c i) t -> p c t i", i=4),
+                result[:, :, cols].rearrange("p t (c i) -> p c t i", i=4),
+            )
             nc.vector.quantize_mx(out_codes[:, cols].bitcast(FP8X4), out_scales[:, cols], rounded[:, cols, :].rearrange("p c t -> p (c t)"))
             nc.sync.dma_start(out_words[:, cols], out_codes[:, cols].bitcast(I32))
         for q in range(QUADS):

@@ -23,7 +23,7 @@ HALF = COLS // 2
 LIST_ROWS = 16
 QUADS = 4
 SPARE = 16
-Y_ON_VECTOR = (1,)
+Y_ON_VECTOR = (1, 3)
 
 FLOPS = 4 * 2 * 512 * 512 * 512
 
@@ -63,18 +63,18 @@ def tile_picked_jkeyliftghopmhopg_none_po_kernel(
             nc.sync.dma_start(raw[:].bitcast(I32), words[0].bitcast(I32))
             return raw
 
-        def deal_fp4_words(name, raw, tiles, tag=None):
+        def deal_fp4_words(name, raw, tiles, engine, tag=None):
             count = tiles.stop - tiles.start
             dealt = new(name, [P, 2 * P * count], U8, tag=tag)
-            nc.vector.tensor_copy(
+            engine.tensor_copy(
                 dealt[:].rearrange("p (t m b) -> p t m b", t=count, b=2),
                 raw[:].rearrange("p (m t b) -> p t m b", t=PACK, b=2)[:, tiles],
             )
             return [dealt[:, 2 * P * i : 2 * P * (i + 1)] for i in range(count)]
 
-        def deal_columns(name, raw, dtype, tag=None):
-            dealt = new(name, [P, COLS], dtype, tag=tag)
-            nc.vector.tensor_copy(
+        def deal_columns(name, raw, engine, tag=None):
+            dealt = new(name, [P, COLS], U8, tag=tag)
+            engine.tensor_copy(
                 dealt[:].rearrange("p (t m) -> p t m", t=PACK),
                 raw.rearrange("p (m t) -> p t m", t=PACK),
             )
@@ -110,9 +110,9 @@ def tile_picked_jkeyliftghopmhopg_none_po_kernel(
 
         xa_scales = gather_codes("xa_scales", x_scale_table[:], offs_l, U8)
         xa_codes = gather_codes("xa_codes", x_table[:], offs_l, U32)
-        w1_codes = deal_fp4_words("w1_codes_first", w1_raw, slice(0, 1))
-        w1_sc = deal_columns("w1_sc", w1_scale_raw[:], U8)
-        w1_codes = w1_codes + deal_fp4_words("w1_codes_rest", w1_raw, slice(1, PACK), tag="w1_scale_raw")
+        w1_codes = deal_fp4_words("w1_codes_first", w1_raw, slice(0, 1), nc.vector)
+        w1_sc = deal_columns("w1_sc", w1_scale_raw[:], nc.vector)
+        w1_codes = w1_codes + deal_fp4_words("w1_codes_rest", w1_raw, slice(1, PACK), nc.vector, tag="w1_scale_raw")
 
         def fp4_product(acc, codes, scales, t, moving, moving_scales, start, stop):
             nc.tensor.matmul_mx(
@@ -125,33 +125,39 @@ def tile_picked_jkeyliftghopmhopg_none_po_kernel(
                 stop=stop,
             )
 
-        y_acc = []
-        for t in range(PACK):
+        whole = slice(0, COLS)
+        halves = [slice(0, HALF), slice(HALF, COLS)]
+
+        y_first = []
+        for cols, tag in zip(halves, ("bank_a0", "bank_b3")):
+            acc = psum.tile([P, COLS], F32, name="y_first_" + tag, tag=tag)
+            fp4_product(acc[:, cols], w1_codes, w1_sc, 0, xa_codes[:, cols], xa_scales[:, cols], True, True)
+            y_first.append(acc)
+        y_acc = [None]
+        for t in range(1, PACK):
             acc = psum.tile([P, COLS], F32, name=f"y_acc{t}", tag=f"bank_a{t}")
             fp4_product(acc[:], w1_codes, w1_sc, t, xa_codes[:], xa_scales[:], True, True)
             y_acc.append(acc)
 
         pa = new("pa", [P, PACK, HALF], F32)
         pb = new("pb", [P, PACK, HALF], F32)
-        def differences(name, tiles, tag=None):
-            count = tiles.stop - tiles.start
-            diff = new(name, [P, count, HALF], F32, tag=tag)
-            nc.vector.tensor_tensor(diff[:], pb[:, tiles, :], pa[:, tiles, :], ALU.subtract)
-            return [diff[:, i, :] for i in range(count)]
+        ra = new("ra", [P, PACK, HALF], F32)
 
         for t in range(PACK):
             y_t = new(f"y{t}", [P, COLS], F32)
-            if t in Y_ON_VECTOR:
+            if t == 0:
+                nc.scalar.activation(y_t[:, halves[0]], y_first[0][:, halves[0]], COPY)
+                nc.vector.tensor_copy(y_t[:, halves[1]], y_first[1][:, halves[1]])
+            elif t in Y_ON_VECTOR:
                 nc.vector.tensor_copy(y_t[:], y_acc[t][:])
             else:
                 nc.scalar.activation(y_t[:], y_acc[t][:], COPY)
             nc.scalar.activation(pa[:, t, :], y_t[:].indirect(n1_l[:]), COPY)
             nc.scalar.activation(pb[:, t, :], y_t[:].indirect(n2_l[:]), COPY)
-            if t == 0:
-                ra = differences("ra_first", slice(0, 1))
+            (nc.vector if t == 0 else nc.gpsimd).tensor_tensor(ra[:, t, :], pb[:, t, :], pa[:, t, :], ALU.subtract)
 
         key_scales_picked = gather_codes("key_scales_picked", d_scale_table[:], kidx_l, U8)
-        key_scales_dealt = deal_columns("key_scales_dealt", key_scales_picked[:], U8)
+        key_scales_dealt = deal_columns("key_scales_dealt", key_scales_picked[:], nc.vector)
         for r in range(4):
             src_row = LIST_ROWS * (r // 2) + r % 2
             nc.sync.dma_start(key_scales[r:P:32, :].bitcast(I32), key_scales_dealt[src_row:P:32, :].bitcast(I32))
@@ -199,10 +205,7 @@ def tile_picked_jkeyliftghopmhopg_none_po_kernel(
 
         rb = new("rb", [P, PACK, HALF], F32, tag="xb_codes")
         nc.vector.scalar_tensor_tensor(rb[:], pa[:], 0.5, pb[:], ALU.mult, ALU.max)
-        ra = ra + differences("ra_rest", slice(1, PACK), tag="key_codes")
-
-        whole = slice(0, COLS)
-        halves = [slice(0, HALF), slice(HALF, COLS)]
+        w2_codes = deal_fp4_words("w2_codes", w2_raw, slice(0, PACK), nc.vector, tag="key_codes")
 
         def quantise(name, pairs, spans):
             grouped = new(name + "_grouped", [P, COLS, PACK], BF16)
@@ -233,74 +236,91 @@ def tile_picked_jkeyliftghopmhopg_none_po_kernel(
             nc.vector.tensor_tensor(larger[:], st[:], st_n4[:], ALU.max)
             nc.vector.tensor_scalar(z2_pairs[:, t // 2, :, t % 2], larger[:], gk_t[:, t : t + 1], None, ALU.mult)
 
-        w3_codes = deal_fp4_words("w3_codes", w3_raw, slice(0, PACK), tag="key_picked")
-        w3_sc = deal_columns("w3_sc", w3_scale_raw[:], U8, tag="xb_scales")
-        w2_codes = deal_fp4_words("w2_codes", w2_raw, slice(0, PACK), tag="mb0")
-        w2_sc = deal_columns("w2_sc", w2_scale_raw[:], U8, tag="key_scales")
+        w3_codes = deal_fp4_words("w3_codes", w3_raw, slice(0, PACK), nc.gpsimd, tag="key_picked")
+        w3_sc = deal_columns("w3_sc", w3_scale_raw[:], nc.gpsimd, tag="w3_raw")
+        w2_sc = deal_columns("w2_sc", w2_scale_raw[:], nc.vector, tag="mb0")
         z2_codes, z2_scales = quantise("z2", z2_pairs, [whole])
 
         z_pairs = new("z_pairs", [P, 2, COLS, 2], BF16, tag="pairs")
         for t in range(PACK):
-            dt = new(f"dt{t}", [P, COLS], F32, tag=f"window{t}" if t > 0 else None)
-            nc.scalar.activation(dt[:].indirect(n1_l[:]), ra[t], COPY)
+            dt = new(f"dt{t}", [P, COLS], F32, tag=f"window{t}" if t > 1 else None)
+            nc.scalar.activation(dt[:].indirect(n1_l[:]), ra[:, t, :], COPY)
             nc.scalar.activation(dt[:].indirect(n2_l[:]), rb[:, t, :], COPY)
             for cols in halves if t == PACK - 1 else [whole]:
                 nc.vector.tensor_scalar(z_pairs[:, t // 2, cols, t % 2], dt[:, cols], gn_t[:, t : t + 1], None, ALU.mult)
         z_codes, z_scales = quantise("z", z_pairs, halves)
 
-        h_acc = []
-        for t in range(PACK):
-            acc = psum.tile([P, COLS], F32, name=f"h_acc{t}", tag=f"bank_a{t}")
-            fp4_product(acc[:], w3_codes, w3_sc, t, z2_codes[:], z2_scales[:], True, False)
-            h_acc.append(acc)
-        for t in range(PACK):
-            for cols in halves:
-                fp4_product(h_acc[t][:, cols], w2_codes, w2_sc, t, z_codes[:, cols], z_scales[:, cols], False, cols == halves[-1])
+        h_first = [psum.tile([P, COLS], F32, name="h_first_" + tag, tag=tag) for tag in ("bank_a0", "bank_b0")]
+        h_acc = [None] + [psum.tile([P, COLS], F32, name=f"h_acc{t}", tag=f"bank_a{t}") for t in range(1, PACK)]
+        for acc, cols in zip(h_first, halves):
+            fp4_product(acc[:, cols], w3_codes, w3_sc, 0, z2_codes[:, cols], z2_scales[:, cols], True, False)
+        for t in range(1, PACK):
+            fp4_product(h_acc[t][:], w3_codes, w3_sc, t, z2_codes[:], z2_scales[:], True, False)
+        for acc, cols in zip(h_first, halves):
+            fp4_product(acc[:, cols], w2_codes, w2_sc, 0, z_codes[:, cols], z_scales[:, cols], False, True)
+        for t in range(1, PACK):
+            fp4_product(h_acc[t][:], w2_codes, w2_sc, t, z_codes[:], z_scales[:], False, True)
 
         result = new("result", [P, PACK, COLS], F32)
         rounded = new("rounded", [P, COLS, PACK], BF16)
         out_rows = out_0.rearrange("(p t) c -> p t c", t=PACK)
         h, st2 = [], []
-        for t in range(PACK):
+
+        def copy_h(t):
             h_t = new(f"h{t}", [P, COLS], F32)
-            nc.vector.tensor_copy(h_t[:], h_acc[t][:])
+            if t == 0:
+                for acc, cols in zip(h_first, halves):
+                    nc.vector.tensor_copy(h_t[:, cols], acc[:, cols])
+            else:
+                nc.vector.tensor_copy(h_t[:], h_acc[t][:])
             h.append(h_t)
+
+        for t in range(PACK - 1):
+            copy_h(t)
         out_codes = new("out_codes", [P, COLS], U32)
         out_scales = new("out_scales", [P, COLS], U8)
         out_words = out_1[0].rearrange("p n t -> p (n t)").bitcast(I32)
 
-        def subtract(t, cols, fetched):
-            nc.vector.tensor_tensor(result[:, t, cols], st2[t][:, cols], fetched, ALU.subtract)
-            nc.sync.dma_start(out_rows[:, t, cols], result[:, t, cols])
+        def subtract(engine, t, cols, fetched):
+            engine.tensor_tensor(result[:, t, cols], st2[t][:, cols], fetched[:, cols], ALU.subtract)
 
-        def fetch_n6(fetched, t, i):
-            looked_up = st2[t][:].indirect(entries(n6_l, i * HALF, HALF))
-            if t == 0:
-                nc.vector.tensor_copy(fetched, looked_up)
-            else:
-                nc.scalar.activation(fetched, looked_up, COPY)
+        def fetch_n6(t, fetch):
+            fetched = new(f"st2_n6_{t}", [P, COLS], F32)
+            for i in range(2):
+                fetch(fetched[:, halves[i]], st2[t][:].indirect(entries(n6_l, i * HALF, HALF)))
+            return fetched
+
+        def scalar_fetch(dst, looked_up):
+            nc.scalar.activation(dst, looked_up, COPY)
 
         for t in range(PACK):
             gate = new(f"gate{t}", [P, COLS], F32)
             for i in range(2):
                 nc.scalar.activation(gate[:, halves[i]], h[t][:].indirect(entries(n5_l, i * HALF, HALF)), SIGMOID)
             st2_t = new(f"st2_{t}", [P, COLS], F32)
-            nc.vector.tensor_tensor(st2_t[:], h[t][:], gate[:], ALU.mult)
+            if t == 1:
+                nc.gpsimd.tensor_tensor(st2_t[:], h[t][:], gate[:], ALU.mult)
+            else:
+                nc.vector.tensor_tensor(st2_t[:], (h if t == 0 else h_acc)[t][:], gate[:], ALU.mult)
             st2.append(st2_t)
             if t == 0:
-                fetched_first = new("st2_n6_first", [P, COLS], F32)
-                for i in range(2):
-                    fetch_n6(fetched_first[:, halves[i]], 0, i)
-        subtract(0, whole, fetched_first[:])
-        for i, cols in enumerate(halves):
-            fetched = new(f"st2_n6_half{i}", [P, PACK - 1, HALF], F32, tag="gate3" if i == 1 else None)
-            for t in range(1, PACK):
-                fetch_n6(fetched[:, t - 1, :], t, i)
-                subtract(t, cols, fetched[:, t - 1, :])
-            nc.vector.tensor_copy(
+                copy_h(PACK - 1)
+            if t in (0, 2):
+                fetched_early = fetch_n6(t // 2, nc.vector.tensor_copy)
+                for cols in halves:
+                    subtract(nc.gpsimd, t // 2, cols, fetched_early)
+                nc.sync.dma_start(out_rows[:, t // 2, :], result[:, t // 2, :])
+        subtract(nc.vector, 2, whole, fetch_n6(2, scalar_fetch))
+        fetched_last = fetch_n6(3, scalar_fetch)
+        for cols in halves:
+            subtract(nc.vector, 3, cols, fetched_last)
+        nc.sync.dma_start(out_rows[:, 2:, :], result[:, 2:, :])
+        for cols, copy in zip(halves, (nc.scalar.copy, nc.vector.tensor_copy)):
+            copy(
                 rounded[:, cols, :].rearrange("p (c i) t -> p c t i", i=4),
                 result[:, :, cols].rearrange("p t (c i) -> p c t i", i=4),
             )
+        for cols in reversed(halves):
             nc.vector.quantize_mx(out_codes[:, cols].bitcast(FP8X4), out_scales[:, cols], rounded[:, cols, :].rearrange("p c t -> p (c t)"))
             nc.sync.dma_start(out_words[:, cols], out_codes[:, cols].bitcast(I32))
         for q in range(QUADS):

@@ -16,13 +16,18 @@ SIGMOID = mybir.ActivationFunctionType.Sigmoid
 
 P = 128
 PACK = 4
+LAST = PACK - 1
 COLS = 512
+HALF = COLS // 2
 TOKENS = 1024
 CODEWORDS = 2048
-HALF = COLS // 2
-LIST_ROWS = 16
+GROUP = 16
 QUADS = 4
+QUAD = P // QUADS
+SCALE_ROWS = 4
+RUN_ROWS = 2
 SPARE = 16
+S_FACTOR = 0.0625
 Y_ON_VECTOR = (1, 3)
 
 FLOPS = 4 * 2 * 512 * 512 * 512
@@ -33,13 +38,15 @@ def tile_picked_jkeyliftghopmhopg_none_po_kernel(
     w3_words, w3_scales, offs, kidx, two, n1, n2, n3, n4, n5, n6, out_0, out_1, out_2,
 ):
     nc = tc.nc
+    whole = slice(0, COLS)
+    halves = [slice(0, HALF), slice(HALF, COLS)]
 
     with ExitStack() as ctx:
         keep = ctx.enter_context(tc.tile_pool(name="keep", bufs=1))
         psum = ctx.enter_context(tc.psum_pool(name="psum", bufs=1))
 
-        def new(name, shape, dtype, tag=None):
-            return keep.tile(shape, dtype, name=name, tag=tag or name, align_bytes=64)
+        def new(name, shape, dtype, reuse=None):
+            return keep.tile(shape, dtype, name=name, tag=reuse or name, align_bytes=64)
 
         def load_list(name, src):
             lst = new(name, list(src.shape), U16)
@@ -47,72 +54,46 @@ def tile_picked_jkeyliftghopmhopg_none_po_kernel(
             return lst
 
         def entries(lst, start, count):
-            return lst[:, start // LIST_ROWS : (start + count) // LIST_ROWS]
+            return lst[:, start // GROUP : (start + count) // GROUP]
 
-        def zeroed_bytes(name, width, engine):
-            plane = new(name, [P, width], U8)
-            engine.memset(plane[:].bitcast(I32), 0)
-            return plane
+        def zeroed_bytes(name, width):
+            tile = new(name, [P, width], U8)
+            nc.gpsimd.memset(tile[:].bitcast(I32), 0)
+            return tile
 
-        def load_scale_rows(plane, scales):
+        def load_scale_rows(tile, scales):
             for q in range(QUADS):
-                nc.sync.dma_start(plane[32 * q : 32 * q + 4, :].bitcast(I32), scales[0, 4 * q : 4 * q + 4, :].bitcast(I32))
+                nc.sync.dma_start(
+                    tile[QUAD * q : QUAD * q + SCALE_ROWS, :].bitcast(I32),
+                    scales[0, SCALE_ROWS * q : SCALE_ROWS * (q + 1), :].bitcast(I32),
+                )
 
         def load_fp4_words(name, words):
             raw = new(name, [P, 2 * COLS], U8)
             nc.sync.dma_start(raw[:].bitcast(I32), words[0].bitcast(I32))
             return raw
 
-        def deal_fp4_words(name, raw, tiles, engine, tag=None):
-            count = tiles.stop - tiles.start
-            dealt = new(name, [P, 2 * P * count], U8, tag=tag)
+        def deal_fp4_words(name, raw, row_tiles, engine, reuse=None):
+            count = row_tiles.stop - row_tiles.start
+            dealt = new(name, [P, 2 * P * count], U8, reuse=reuse)
             engine.tensor_copy(
                 dealt[:].rearrange("p (t m b) -> p t m b", t=count, b=2),
-                raw[:].rearrange("p (m t b) -> p t m b", t=PACK, b=2)[:, tiles],
+                raw[:].rearrange("p (m t b) -> p t m b", t=PACK, b=2)[:, row_tiles],
             )
             return [dealt[:, 2 * P * i : 2 * P * (i + 1)] for i in range(count)]
 
-        def deal_columns(name, raw, engine, tag=None):
-            dealt = new(name, [P, COLS], U8, tag=tag)
+        def deal_scale_bytes(name, raw, engine, reuse=None):
+            dealt = new(name, [P, COLS], U8, reuse=reuse)
             engine.tensor_copy(
                 dealt[:].rearrange("p (t m) -> p t m", t=PACK),
-                raw.rearrange("p (m t) -> p t m", t=PACK),
+                raw[:].rearrange("p (m t) -> p t m", t=PACK),
             )
             return dealt
 
-        def gather_codes(name, table, lst, dtype):
+        def gather_packed(name, table, lst, dtype):
             picked = new(name, [P, COLS], dtype)
-            nc.vector.tensor_copy(picked[:], table.indirect(lst[:]))
+            nc.vector.tensor_copy(picked[:], table[:].indirect(lst[:]))
             return picked
-
-        x_scale_table = zeroed_bytes("x_scale_table", TOKENS, nc.gpsimd)
-        w1_scale_raw = zeroed_bytes("w1_scale_raw", COLS, nc.gpsimd)
-        d_scale_table = zeroed_bytes("d_scale_table", CODEWORDS, nc.gpsimd)
-        key_scales = zeroed_bytes("key_scales", COLS, nc.gpsimd)
-        w2_scale_raw = zeroed_bytes("w2_scale_raw", COLS, nc.gpsimd)
-        w3_scale_raw = zeroed_bytes("w3_scale_raw", COLS, nc.gpsimd)
-
-        offs_l = load_list("offs_l", offs)
-        load_scale_rows(x_scale_table, x_scales)
-        x_table = new("x_table", [P, TOKENS], U32)
-        nc.sync.dma_start(x_table[:].bitcast(I32), x_words[0].rearrange("p n t -> p (n t)").bitcast(I32))
-        w1_raw = load_fp4_words("w1_raw", w1_words)
-        load_scale_rows(w1_scale_raw, w1_scales)
-        kidx_l = load_list("kidx_l", kidx)
-        for e in range(2):
-            nc.sync.dma_start(d_scale_table[e:P:LIST_ROWS, :].bitcast(I32), d_scales[0, e:16:2, :].bitcast(I32))
-        n1_l = load_list("n1_l", n1)
-        n2_l = load_list("n2_l", n2)
-        two_l = load_list("two_l", two)
-        d_table = new("d_table", [P, CODEWORDS], U32)
-        nc.sync.dma_start(d_table[:].bitcast(I32), d_words[0].rearrange("p n t -> p (n t)").bitcast(I32))
-        n3_l = load_list("n3_l", n3)
-
-        xa_scales = gather_codes("xa_scales", x_scale_table[:], offs_l, U8)
-        xa_codes = gather_codes("xa_codes", x_table[:], offs_l, U32)
-        w1_codes = deal_fp4_words("w1_codes_first", w1_raw, slice(0, 1), nc.vector)
-        w1_sc = deal_columns("w1_sc", w1_scale_raw[:], nc.vector)
-        w1_codes = w1_codes + deal_fp4_words("w1_codes_rest", w1_raw, slice(1, PACK), nc.vector, tag="w1_scale_raw")
 
         def fp4_product(acc, codes, scales, t, moving, moving_scales, start, stop):
             nc.tensor.matmul_mx(
@@ -125,24 +106,66 @@ def tile_picked_jkeyliftghopmhopg_none_po_kernel(
                 stop=stop,
             )
 
-        whole = slice(0, COLS)
-        halves = [slice(0, HALF), slice(HALF, COLS)]
+        def quantise(name, pairs, spans):
+            grouped = new(name + "_grouped", [P, COLS, PACK], BF16)
+            grouped_words = grouped[:].rearrange("p c t -> p (c t)").bitcast(I32).rearrange("p (c u) -> p c u", u=2)
+            pair_words = pairs[:].rearrange("p u c e -> p u (c e)").bitcast(I32).rearrange("p u c -> p c u")
+            codes = new(name + "_codes", [P, COLS], U32)
+            scales = new(name + "_scales", [P, COLS], U8)
+            for cols in spans:
+                nc.vector.tensor_copy(grouped_words[:, cols, :], pair_words[:, cols, :])
+            for cols in spans:
+                nc.vector.quantize_mx(
+                    codes[:, cols].bitcast(FP8X4), scales[:, cols], grouped[:, cols, :].rearrange("p c t -> p (c t)")
+                )
+            return codes, scales
+
+        x_scale_table = zeroed_bytes("x_scale_table", TOKENS)
+        w1_scale_raw = zeroed_bytes("w1_scale_raw", COLS)
+        d_scale_table = zeroed_bytes("d_scale_table", CODEWORDS)
+        key_scales = zeroed_bytes("key_scales", COLS)
+        w2_scale_raw = zeroed_bytes("w2_scale_raw", COLS)
+        w3_scale_raw = zeroed_bytes("w3_scale_raw", COLS)
+
+        offs_l = load_list("offs_l", offs)
+        load_scale_rows(x_scale_table, x_scales)
+        x_table = new("x_table", [P, TOKENS], U32)
+        nc.sync.dma_start(x_table[:].bitcast(I32), x_words[0].rearrange("p n t -> p (n t)").bitcast(I32))
+        w1_raw = load_fp4_words("w1_raw", w1_words)
+        load_scale_rows(w1_scale_raw, w1_scales)
+        kidx_l = load_list("kidx_l", kidx)
+        for e in range(RUN_ROWS):
+            nc.sync.dma_start(
+                d_scale_table[e:P:GROUP, :].bitcast(I32),
+                d_scales[0, e : QUADS * SCALE_ROWS : RUN_ROWS, :].bitcast(I32),
+            )
+        n1_l = load_list("n1_l", n1)
+        n2_l = load_list("n2_l", n2)
+        two_l = load_list("two_l", two)
+        d_table = new("d_table", [P, CODEWORDS], U32)
+        nc.sync.dma_start(d_table[:].bitcast(I32), d_words[0].rearrange("p n t -> p (n t)").bitcast(I32))
+        n3_l = load_list("n3_l", n3)
+
+        x_idx_scales = gather_packed("x_idx_scales", x_scale_table, offs_l, U8)
+        x_idx_codes = gather_packed("x_idx_codes", x_table, offs_l, U32)
+        w1_codes = deal_fp4_words("w1_codes_first", w1_raw, slice(0, 1), nc.vector)
+        w1_scales_dealt = deal_scale_bytes("w1_scales_dealt", w1_scale_raw, nc.vector)
+        w1_codes = w1_codes + deal_fp4_words("w1_codes_rest", w1_raw, slice(1, PACK), nc.vector, reuse="w1_scale_raw")
 
         y_first = []
-        for cols, tag in zip(halves, ("bank_a0", "bank_b3")):
-            acc = psum.tile([P, COLS], F32, name="y_first_" + tag, tag=tag)
-            fp4_product(acc[:, cols], w1_codes, w1_sc, 0, xa_codes[:, cols], xa_scales[:, cols], True, True)
+        for cols, bank in zip(halves, ("bank_a0", f"bank_b{LAST}")):
+            acc = psum.tile([P, COLS], F32, name="y_first_" + bank, tag=bank)
+            fp4_product(acc[:, cols], w1_codes, w1_scales_dealt, 0, x_idx_codes[:, cols], x_idx_scales[:, cols], True, True)
             y_first.append(acc)
-        y_acc = [None]
+        y_acc = {}
         for t in range(1, PACK):
             acc = psum.tile([P, COLS], F32, name=f"y_acc{t}", tag=f"bank_a{t}")
-            fp4_product(acc[:], w1_codes, w1_sc, t, xa_codes[:], xa_scales[:], True, True)
-            y_acc.append(acc)
+            fp4_product(acc[:], w1_codes, w1_scales_dealt, t, x_idx_codes[:], x_idx_scales[:], True, True)
+            y_acc[t] = acc
 
         pa = new("pa", [P, PACK, HALF], F32)
         pb = new("pb", [P, PACK, HALF], F32)
         ra = new("ra", [P, PACK, HALF], F32)
-
         for t in range(PACK):
             y_t = new(f"y{t}", [P, COLS], F32)
             if t == 0:
@@ -156,19 +179,19 @@ def tile_picked_jkeyliftghopmhopg_none_po_kernel(
             nc.scalar.activation(pb[:, t, :], y_t[:].indirect(n2_l[:]), COPY)
             (nc.vector if t == 0 else nc.gpsimd).tensor_tensor(ra[:, t, :], pb[:, t, :], pa[:, t, :], ALU.subtract)
 
-        key_scales_picked = gather_codes("key_scales_picked", d_scale_table[:], kidx_l, U8)
-        key_scales_dealt = deal_columns("key_scales_dealt", key_scales_picked[:], nc.vector)
-        for r in range(4):
-            src_row = LIST_ROWS * (r // 2) + r % 2
-            nc.sync.dma_start(key_scales[r:P:32, :].bitcast(I32), key_scales_dealt[src_row:P:32, :].bitcast(I32))
-        xb_scales = gather_codes("xb_scales", x_scale_table[:], two_l, U8)
-        key_picked = gather_codes("key_picked", d_table[:], kidx_l, U32)
+        key_scales_picked = gather_packed("key_scales_picked", d_scale_table, kidx_l, U8)
+        key_scales_dealt = deal_scale_bytes("key_scales_dealt", key_scales_picked, nc.vector)
+        for r in range(SCALE_ROWS):
+            gathered_on = GROUP * (r // RUN_ROWS) + r % RUN_ROWS
+            nc.sync.dma_start(key_scales[r:P:QUAD, :].bitcast(I32), key_scales_dealt[gathered_on:P:QUAD, :].bitcast(I32))
+        x_two_scales = gather_packed("x_two_scales", x_scale_table, two_l, U8)
+        key_picked = gather_packed("key_picked", d_table, kidx_l, U32)
         key_codes = new("key_codes", [P, COLS], I32)
         nc.vector.tensor_copy(
             key_codes[:].rearrange("p (t m) -> p m t", t=PACK),
             key_picked[:].bitcast(I32).rearrange("p (m t) -> p m t", t=PACK),
         )
-        xb_codes = gather_codes("xb_codes", x_table[:], two_l, U32)
+        x_two_codes = gather_packed("x_two_codes", x_table, two_l, U32)
 
         n4_l = load_list("n4_l", n4)
         gn_t = new("gn_t", [P, PACK], F32)
@@ -189,8 +212,8 @@ def tile_picked_jkeyliftghopmhopg_none_po_kernel(
                 acc[:],
                 lhsT=key_codes[:, P * t : P * (t + 1)].bitcast(FP8X4),
                 lhsT_scale=key_scales[:, P * t : P * (t + 1)],
-                rhs=xb_codes[:].bitcast(FP8X4),
-                rhs_scale=xb_scales[:],
+                rhs=x_two_codes[:].bitcast(FP8X4),
+                rhs_scale=x_two_scales[:],
                 start=True,
                 stop=True,
             )
@@ -198,68 +221,56 @@ def tile_picked_jkeyliftghopmhopg_none_po_kernel(
 
         s = []
         for t in range(PACK):
-            s_t = new(f"s{t}", [P, COLS + SPARE], F32, tag=f"window{t}")
+            s_t = new(f"s{t}", [P, COLS + SPARE], F32)
             nc.gpsimd.memset(s_t[:, COLS:], 0.0)
-            nc.vector.tensor_scalar(s_t[:, :COLS], s_acc[t][:], 0.0625, None, ALU.mult)
+            nc.vector.tensor_scalar(s_t[:, :COLS], s_acc[t][:], S_FACTOR, None, ALU.mult)
             s.append(s_t)
 
-        rb = new("rb", [P, PACK, HALF], F32, tag="xb_codes")
+        rb = new("rb", [P, PACK, HALF], F32, reuse="x_two_codes")
         nc.vector.scalar_tensor_tensor(rb[:], pa[:], 0.5, pb[:], ALU.mult, ALU.max)
-        w2_codes = deal_fp4_words("w2_codes", w2_raw, slice(0, PACK), nc.vector, tag="key_codes")
 
-        def quantise(name, pairs, spans):
-            grouped = new(name + "_grouped", [P, COLS, PACK], BF16)
-            grouped_words = grouped[:].rearrange("p c t -> p (c t)").bitcast(I32).rearrange("p (c u) -> p c u", u=2)
-            pair_words = pairs[:].rearrange("p u c e -> p u (c e)").bitcast(I32).rearrange("p u c -> p c u")
-            codes = new(name + "_codes", [P, COLS], U32)
-            scales = new(name + "_scales", [P, COLS], U8)
-            for cols in spans:
-                nc.vector.tensor_copy(grouped_words[:, cols, :], pair_words[:, cols, :])
-            for cols in spans:
-                nc.vector.quantize_mx(codes[:, cols].bitcast(FP8X4), scales[:, cols], grouped[:, cols, :].rearrange("p c t -> p (c t)"))
-            return codes, scales
-
-        z2_pairs = new("z2_pairs", [P, 2, COLS, 2], BF16, tag="pairs")
+        z2_pairs = new("z2_pairs", [P, 2, COLS, 2], BF16)
         for t in range(PACK):
-            s_t = s[t]
             mb = new(f"mb{t}", [P, 2 * COLS], F32)
             for i in range(2):
-                nc.scalar.activation(mb[:, i * COLS : (i + 1) * COLS], s_t[:].indirect(entries(n3_l, i * COLS, COLS)), COPY)
-            mx = new(f"mx{t}", [P, COLS], F32, tag="mx")
+                nc.scalar.activation(mb[:, i * COLS : (i + 1) * COLS], s[t][:].indirect(entries(n3_l, i * COLS, COLS)), COPY)
+            mx = new(f"mx{t}", [P, COLS], F32, reuse="mx")
             nc.vector.tensor_tensor(mx[:], mb[:, 0 : 2 * COLS : 2], mb[:, 1 : 2 * COLS : 2], ALU.max)
             st = new(f"st{t}", [P, COLS], F32)
-            nc.vector.scalar_tensor_tensor(st[:], s_acc[t][:], 0.0625, mx[:], ALU.mult, ALU.subtract)
+            nc.vector.scalar_tensor_tensor(st[:], s_acc[t][:], S_FACTOR, mx[:], ALU.mult, ALU.subtract)
             st_n4 = new(f"st_n4_{t}", [P, COLS], F32)
-            for i in range(2):
-                nc.vector.tensor_copy(st_n4[:, i * HALF : (i + 1) * HALF], st[:].indirect(entries(n4_l, i * HALF, HALF)))
+            for i, cols in enumerate(halves):
+                nc.vector.tensor_copy(st_n4[:, cols], st[:].indirect(entries(n4_l, i * HALF, HALF)))
             larger = new(f"larger{t}", [P, COLS], F32)
             nc.vector.tensor_tensor(larger[:], st[:], st_n4[:], ALU.max)
             nc.vector.tensor_scalar(z2_pairs[:, t // 2, :, t % 2], larger[:], gk_t[:, t : t + 1], None, ALU.mult)
 
-        w3_codes = deal_fp4_words("w3_codes", w3_raw, slice(0, PACK), nc.gpsimd, tag="key_picked")
-        w3_sc = deal_columns("w3_sc", w3_scale_raw[:], nc.gpsimd, tag="w3_raw")
-        w2_sc = deal_columns("w2_sc", w2_scale_raw[:], nc.vector, tag="mb0")
+        w3_codes = deal_fp4_words("w3_codes", w3_raw, slice(0, PACK), nc.gpsimd, reuse="key_picked")
+        w3_scales_dealt = deal_scale_bytes("w3_scales_dealt", w3_scale_raw, nc.gpsimd, reuse="w3_raw")
+        w2_scales_dealt = deal_scale_bytes("w2_scales_dealt", w2_scale_raw, nc.gpsimd, reuse="larger0")
+        w2_codes = deal_fp4_words("w2_codes_low", w2_raw, slice(0, 2), nc.gpsimd, reuse="larger1")
+        w2_codes = w2_codes + deal_fp4_words("w2_codes_high", w2_raw, slice(2, PACK), nc.gpsimd, reuse="larger2")
         z2_codes, z2_scales = quantise("z2", z2_pairs, [whole])
 
-        z_pairs = new("z_pairs", [P, 2, COLS, 2], BF16, tag="pairs")
+        z_pairs = new("z_pairs", [P, 2, COLS, 2], BF16, reuse="z2_pairs")
         for t in range(PACK):
-            dt = new(f"dt{t}", [P, COLS], F32, tag=f"window{t}" if t > 1 else None)
+            dt = new(f"dt{t}", [P, COLS], F32, reuse=f"s{t}" if t > 1 else None)
             nc.scalar.activation(dt[:].indirect(n1_l[:]), ra[:, t, :], COPY)
             nc.scalar.activation(dt[:].indirect(n2_l[:]), rb[:, t, :], COPY)
-            for cols in halves if t == PACK - 1 else [whole]:
+            for cols in halves if t == LAST else [whole]:
                 nc.vector.tensor_scalar(z_pairs[:, t // 2, cols, t % 2], dt[:, cols], gn_t[:, t : t + 1], None, ALU.mult)
         z_codes, z_scales = quantise("z", z_pairs, halves)
 
-        h_first = [psum.tile([P, COLS], F32, name="h_first_" + tag, tag=tag) for tag in ("bank_a0", "bank_b0")]
-        h_acc = [None] + [psum.tile([P, COLS], F32, name=f"h_acc{t}", tag=f"bank_a{t}") for t in range(1, PACK)]
+        h_first = [psum.tile([P, COLS], F32, name="h_first_" + bank, tag=bank) for bank in ("bank_a0", "bank_b0")]
+        h_acc = {t: psum.tile([P, COLS], F32, name=f"h_acc{t}", tag=f"bank_a{t}") for t in range(1, PACK)}
         for acc, cols in zip(h_first, halves):
-            fp4_product(acc[:, cols], w3_codes, w3_sc, 0, z2_codes[:, cols], z2_scales[:, cols], True, False)
+            fp4_product(acc[:, cols], w3_codes, w3_scales_dealt, 0, z2_codes[:, cols], z2_scales[:, cols], True, False)
         for t in range(1, PACK):
-            fp4_product(h_acc[t][:], w3_codes, w3_sc, t, z2_codes[:], z2_scales[:], True, False)
+            fp4_product(h_acc[t][:], w3_codes, w3_scales_dealt, t, z2_codes[:], z2_scales[:], True, False)
         for acc, cols in zip(h_first, halves):
-            fp4_product(acc[:, cols], w2_codes, w2_sc, 0, z_codes[:, cols], z_scales[:, cols], False, True)
+            fp4_product(acc[:, cols], w2_codes, w2_scales_dealt, 0, z_codes[:, cols], z_scales[:, cols], False, True)
         for t in range(1, PACK):
-            fp4_product(h_acc[t][:], w2_codes, w2_sc, t, z_codes[:], z_scales[:], False, True)
+            fp4_product(h_acc[t][:], w2_codes, w2_scales_dealt, t, z_codes[:], z_scales[:], False, True)
 
         result = new("result", [P, PACK, COLS], F32)
         rounded = new("rounded", [P, COLS, PACK], BF16)
@@ -275,53 +286,60 @@ def tile_picked_jkeyliftghopmhopg_none_po_kernel(
                 nc.vector.tensor_copy(h_t[:], h_acc[t][:])
             h.append(h_t)
 
-        for t in range(PACK - 1):
-            copy_h(t)
-        out_codes = new("out_codes", [P, COLS], U32)
-        out_scales = new("out_scales", [P, COLS], U8)
-        out_words = out_1[0].rearrange("p n t -> p (n t)").bitcast(I32)
-
-        def subtract(engine, t, cols, fetched):
-            engine.tensor_tensor(result[:, t, cols], st2[t][:, cols], fetched[:, cols], ALU.subtract)
+        def gated(t, engine, h_source):
+            gate = new(f"gate{t}", [P, COLS], F32)
+            for i, cols in enumerate(halves):
+                nc.scalar.activation(gate[:, cols], h[t][:].indirect(entries(n5_l, i * HALF, HALF)), SIGMOID)
+            st2_t = new(f"st2_{t}", [P, COLS], F32)
+            engine.tensor_tensor(st2_t[:], h_source[:], gate[:], ALU.mult)
+            st2.append(st2_t)
 
         def fetch_n6(t, fetch):
             fetched = new(f"st2_n6_{t}", [P, COLS], F32)
-            for i in range(2):
-                fetch(fetched[:, halves[i]], st2[t][:].indirect(entries(n6_l, i * HALF, HALF)))
+            for i, cols in enumerate(halves):
+                fetch(fetched[:, cols], st2[t][:].indirect(entries(n6_l, i * HALF, HALF)))
             return fetched
 
         def scalar_fetch(dst, looked_up):
             nc.scalar.activation(dst, looked_up, COPY)
 
-        for t in range(PACK):
-            gate = new(f"gate{t}", [P, COLS], F32)
-            for i in range(2):
-                nc.scalar.activation(gate[:, halves[i]], h[t][:].indirect(entries(n5_l, i * HALF, HALF)), SIGMOID)
-            st2_t = new(f"st2_{t}", [P, COLS], F32)
-            if t == 1:
-                nc.gpsimd.tensor_tensor(st2_t[:], h[t][:], gate[:], ALU.mult)
-            else:
-                nc.vector.tensor_tensor(st2_t[:], (h if t == 0 else h_acc)[t][:], gate[:], ALU.mult)
-            st2.append(st2_t)
-            if t == 0:
-                copy_h(PACK - 1)
-            if t in (0, 2):
-                fetched_early = fetch_n6(t // 2, nc.vector.tensor_copy)
-                for cols in halves:
-                    subtract(nc.gpsimd, t // 2, cols, fetched_early)
-                nc.sync.dma_start(out_rows[:, t // 2, :], result[:, t // 2, :])
-        subtract(nc.vector, 2, whole, fetch_n6(2, scalar_fetch))
-        fetched_last = fetch_n6(3, scalar_fetch)
-        for cols in halves:
-            subtract(nc.vector, 3, cols, fetched_last)
+        def subtract(engine, t, spans, fetched):
+            for cols in spans:
+                engine.tensor_tensor(result[:, t, cols], st2[t][:, cols], fetched[:, cols], ALU.subtract)
+
+        def finish_early(t):
+            subtract(nc.gpsimd, t, halves, fetch_n6(t, nc.vector.tensor_copy))
+            nc.sync.dma_start(out_rows[:, t, :], result[:, t, :])
+
+        for t in range(LAST):
+            copy_h(t)
+        out_codes = new("out_codes", [P, COLS], U32)
+        out_scales = new("out_scales", [P, COLS], U8)
+        out_words = out_1[0].rearrange("p n t -> p (n t)").bitcast(I32)
+
+        gated(0, nc.vector, h[0])
+        copy_h(LAST)
+        finish_early(0)
+        gated(1, nc.gpsimd, h[1])
+        gated(2, nc.vector, h_acc[2])
+        finish_early(1)
+        gated(LAST, nc.vector, h_acc[LAST])
+        subtract(nc.vector, 2, [whole], fetch_n6(2, scalar_fetch))
+        subtract(nc.vector, LAST, halves, fetch_n6(LAST, scalar_fetch))
         nc.sync.dma_start(out_rows[:, 2:, :], result[:, 2:, :])
+
         for cols, copy in zip(halves, (nc.scalar.copy, nc.vector.tensor_copy)):
             copy(
                 rounded[:, cols, :].rearrange("p (c i) t -> p c t i", i=4),
                 result[:, :, cols].rearrange("p t (c i) -> p c t i", i=4),
             )
         for cols in reversed(halves):
-            nc.vector.quantize_mx(out_codes[:, cols].bitcast(FP8X4), out_scales[:, cols], rounded[:, cols, :].rearrange("p c t -> p (c t)"))
+            nc.vector.quantize_mx(
+                out_codes[:, cols].bitcast(FP8X4), out_scales[:, cols], rounded[:, cols, :].rearrange("p c t -> p (c t)")
+            )
             nc.sync.dma_start(out_words[:, cols], out_codes[:, cols].bitcast(I32))
         for q in range(QUADS):
-            nc.sync.dma_start(out_2[0, 4 * q : 4 * q + 4, :].bitcast(I32), out_scales[32 * q : 32 * q + 4, :].bitcast(I32))
+            nc.sync.dma_start(
+                out_2[0, SCALE_ROWS * q : SCALE_ROWS * (q + 1), :].bitcast(I32),
+                out_scales[QUAD * q : QUAD * q + SCALE_ROWS, :].bitcast(I32),
+            )

from contextlib import ExitStack

import concourse.mybir as mybir

F32 = mybir.dt.float32
BF16 = mybir.dt.bfloat16
I32 = mybir.dt.int32
U32 = mybir.dt.uint32
U16 = mybir.dt.uint16
U8 = mybir.dt.uint8
FP8X4 = mybir.dt.float8_e4m3fn_x4
FP4X4 = mybir.dt.float4_e2m1fn_x4
ALU = mybir.AluOpType
COPY = mybir.ActivationFunctionType.Copy
SIGMOID = mybir.ActivationFunctionType.Sigmoid

P = 128
PACK = 4
LAST = PACK - 1
COLS = 512
HALF = COLS // 2
TOKENS = 1024
CODEWORDS = 2048
GROUP = 16
QUADS = 4
QUAD = P // QUADS
SCALE_ROWS = 4
RUN_ROWS = 2
SPARE = 16
S_FACTOR = 0.0625
Y_ON_VECTOR = (1, 3)

FLOPS = 4 * 2 * 512 * 512 * 512


def tile_picked_jkeyliftghopmhopg_none_po_kernel(
    tc, x_words, x_scales, w1_words, w1_scales, d_words, d_scales, gn, gk, w2_words, w2_scales,
    w3_words, w3_scales, offs, kidx, two, n1, n2, n3, n4, n5, n6, out_0, out_1, out_2,
):
    nc = tc.nc
    whole = slice(0, COLS)
    halves = [slice(0, HALF), slice(HALF, COLS)]

    with ExitStack() as ctx:
        keep = ctx.enter_context(tc.tile_pool(name="keep", bufs=1))
        psum = ctx.enter_context(tc.psum_pool(name="psum", bufs=1))

        def new(name, shape, dtype, reuse=None):
            return keep.tile(shape, dtype, name=name, tag=reuse or name, align_bytes=64)

        def load_list(name, src):
            lst = new(name, list(src.shape), U16)
            nc.sync.dma_start(lst[:], src)
            return lst

        def entries(lst, start, count):
            return lst[:, start // GROUP : (start + count) // GROUP]

        def zeroed_bytes(name, width):
            tile = new(name, [P, width], U8)
            nc.gpsimd.memset(tile[:].bitcast(I32), 0)
            return tile

        def load_scale_rows(tile, scales):
            for q in range(QUADS):
                nc.sync.dma_start(
                    tile[QUAD * q : QUAD * q + SCALE_ROWS, :].bitcast(I32),
                    scales[0, SCALE_ROWS * q : SCALE_ROWS * (q + 1), :].bitcast(I32),
                )

        def load_fp4_words(name, words):
            raw = new(name, [P, 2 * COLS], U8)
            nc.sync.dma_start(raw[:].bitcast(I32), words[0].bitcast(I32))
            return raw

        def deal_fp4_words(name, raw, row_tiles, engine, reuse=None):
            count = row_tiles.stop - row_tiles.start
            dealt = new(name, [P, 2 * P * count], U8, reuse=reuse)
            engine.tensor_copy(
                dealt[:].rearrange("p (t m b) -> p t m b", t=count, b=2),
                raw[:].rearrange("p (m t b) -> p t m b", t=PACK, b=2)[:, row_tiles],
            )
            return [dealt[:, 2 * P * i : 2 * P * (i + 1)] for i in range(count)]

        def deal_scale_bytes(name, raw, engine, reuse=None):
            dealt = new(name, [P, COLS], U8, reuse=reuse)
            engine.tensor_copy(
                dealt[:].rearrange("p (t m) -> p t m", t=PACK),
                raw[:].rearrange("p (m t) -> p t m", t=PACK),
            )
            return dealt

        def gather_packed(name, table, lst, dtype):
            picked = new(name, [P, COLS], dtype)
            nc.vector.tensor_copy(picked[:], table[:].indirect(lst[:]))
            return picked

        def fp4_product(acc, codes, scales, t, moving, moving_scales, start, stop):
            nc.tensor.matmul_mx(
                acc,
                lhsT=codes[t].bitcast(FP4X4),
                lhsT_scale=scales[:, P * t : P * (t + 1)],
                rhs=moving.bitcast(FP8X4),
                rhs_scale=moving_scales,
                start=start,
                stop=stop,
            )

        def quantise(name, pairs, spans):
            grouped = new(name + "_grouped", [P, COLS, PACK], BF16)
            grouped_words = grouped[:].rearrange("p c t -> p (c t)").bitcast(I32).rearrange("p (c u) -> p c u", u=2)
            pair_words = pairs[:].rearrange("p u c e -> p u (c e)").bitcast(I32).rearrange("p u c -> p c u")
            codes = new(name + "_codes", [P, COLS], U32)
            scales = new(name + "_scales", [P, COLS], U8)
            for cols in spans:
                nc.vector.tensor_copy(grouped_words[:, cols, :], pair_words[:, cols, :])
            for cols in spans:
                nc.vector.quantize_mx(
                    codes[:, cols].bitcast(FP8X4), scales[:, cols], grouped[:, cols, :].rearrange("p c t -> p (c t)")
                )
            return codes, scales

        x_scale_table = zeroed_bytes("x_scale_table", TOKENS)
        w1_scale_raw = zeroed_bytes("w1_scale_raw", COLS)
        d_scale_table = zeroed_bytes("d_scale_table", CODEWORDS)
        key_scales = zeroed_bytes("key_scales", COLS)
        w2_scale_raw = zeroed_bytes("w2_scale_raw", COLS)
        w3_scale_raw = zeroed_bytes("w3_scale_raw", COLS)

        offs_l = load_list("offs_l", offs)
        load_scale_rows(x_scale_table, x_scales)
        x_table = new("x_table", [P, TOKENS], U32)
        nc.sync.dma_start(x_table[:].bitcast(I32), x_words[0].rearrange("p n t -> p (n t)").bitcast(I32))
        w1_raw = load_fp4_words("w1_raw", w1_words)
        load_scale_rows(w1_scale_raw, w1_scales)
        kidx_l = load_list("kidx_l", kidx)
        for e in range(RUN_ROWS):
            nc.sync.dma_start(
                d_scale_table[e:P:GROUP, :].bitcast(I32),
                d_scales[0, e : QUADS * SCALE_ROWS : RUN_ROWS, :].bitcast(I32),
            )
        n1_l = load_list("n1_l", n1)
        n2_l = load_list("n2_l", n2)
        two_l = load_list("two_l", two)
        d_table = new("d_table", [P, CODEWORDS], U32)
        nc.sync.dma_start(d_table[:].bitcast(I32), d_words[0].rearrange("p n t -> p (n t)").bitcast(I32))
        n3_l = load_list("n3_l", n3)

        x_idx_scales = gather_packed("x_idx_scales", x_scale_table, offs_l, U8)
        x_idx_codes = gather_packed("x_idx_codes", x_table, offs_l, U32)
        w1_codes = deal_fp4_words("w1_codes_first", w1_raw, slice(0, 1), nc.vector)
        w1_scales_dealt = deal_scale_bytes("w1_scales_dealt", w1_scale_raw, nc.vector)
        w1_codes = w1_codes + deal_fp4_words("w1_codes_rest", w1_raw, slice(1, PACK), nc.vector, reuse="w1_scale_raw")

        y_first = []
        for cols, bank in zip(halves, ("bank_a0", f"bank_b{LAST}")):
            acc = psum.tile([P, COLS], F32, name="y_first_" + bank, tag=bank)
            fp4_product(acc[:, cols], w1_codes, w1_scales_dealt, 0, x_idx_codes[:, cols], x_idx_scales[:, cols], True, True)
            y_first.append(acc)
        y_acc = {}
        for t in range(1, PACK):
            acc = psum.tile([P, COLS], F32, name=f"y_acc{t}", tag=f"bank_a{t}")
            fp4_product(acc[:], w1_codes, w1_scales_dealt, t, x_idx_codes[:], x_idx_scales[:], True, True)
            y_acc[t] = acc

        pa = new("pa", [P, PACK, HALF], F32)
        pb = new("pb", [P, PACK, HALF], F32)
        ra = new("ra", [P, PACK, HALF], F32)
        for t in range(PACK):
            y_t = new(f"y{t}", [P, COLS], F32)
            if t == 0:
                nc.scalar.activation(y_t[:, halves[0]], y_first[0][:, halves[0]], COPY)
                nc.vector.tensor_copy(y_t[:, halves[1]], y_first[1][:, halves[1]])
            elif t in Y_ON_VECTOR:
                nc.vector.tensor_copy(y_t[:], y_acc[t][:])
            else:
                nc.scalar.activation(y_t[:], y_acc[t][:], COPY)
            nc.scalar.activation(pa[:, t, :], y_t[:].indirect(n1_l[:]), COPY)
            nc.scalar.activation(pb[:, t, :], y_t[:].indirect(n2_l[:]), COPY)
            (nc.vector if t == 0 else nc.gpsimd).tensor_tensor(ra[:, t, :], pb[:, t, :], pa[:, t, :], ALU.subtract)

        key_scales_picked = gather_packed("key_scales_picked", d_scale_table, kidx_l, U8)
        key_scales_dealt = deal_scale_bytes("key_scales_dealt", key_scales_picked, nc.vector)
        for r in range(SCALE_ROWS):
            gathered_on = GROUP * (r // RUN_ROWS) + r % RUN_ROWS
            nc.sync.dma_start(key_scales[r:P:QUAD, :].bitcast(I32), key_scales_dealt[gathered_on:P:QUAD, :].bitcast(I32))
        x_two_scales = gather_packed("x_two_scales", x_scale_table, two_l, U8)
        key_picked = gather_packed("key_picked", d_table, kidx_l, U32)
        key_codes = new("key_codes", [P, COLS], I32)
        nc.vector.tensor_copy(
            key_codes[:].rearrange("p (t m) -> p m t", t=PACK),
            key_picked[:].bitcast(I32).rearrange("p (m t) -> p m t", t=PACK),
        )
        x_two_codes = gather_packed("x_two_codes", x_table, two_l, U32)

        n4_l = load_list("n4_l", n4)
        gn_t = new("gn_t", [P, PACK], F32)
        nc.sync.dma_start(gn_t[:], gn.rearrange("(p t) o -> p (t o)", t=PACK))
        gk_t = new("gk_t", [P, PACK], F32)
        nc.sync.dma_start(gk_t[:], gk.rearrange("(p t) o -> p (t o)", t=PACK))
        w3_raw = load_fp4_words("w3_raw", w3_words)
        load_scale_rows(w3_scale_raw, w3_scales)
        w2_raw = load_fp4_words("w2_raw", w2_words)
        load_scale_rows(w2_scale_raw, w2_scales)
        n5_l = load_list("n5_l", n5)
        n6_l = load_list("n6_l", n6)

        s_acc = []
        for t in range(PACK):
            acc = psum.tile([P, COLS], F32, name=f"s_acc{t}", tag=f"bank_b{t}")
            nc.tensor.matmul_mx(
                acc[:],
                lhsT=key_codes[:, P * t : P * (t + 1)].bitcast(FP8X4),
                lhsT_scale=key_scales[:, P * t : P * (t + 1)],
                rhs=x_two_codes[:].bitcast(FP8X4),
                rhs_scale=x_two_scales[:],
                start=True,
                stop=True,
            )
            s_acc.append(acc)

        s = []
        for t in range(PACK):
            s_t = new(f"s{t}", [P, COLS + SPARE], F32)
            nc.gpsimd.memset(s_t[:, COLS:], 0.0)
            nc.vector.tensor_scalar(s_t[:, :COLS], s_acc[t][:], S_FACTOR, None, ALU.mult)
            s.append(s_t)

        rb = new("rb", [P, PACK, HALF], F32, reuse="x_two_codes")
        nc.vector.scalar_tensor_tensor(rb[:], pa[:], 0.5, pb[:], ALU.mult, ALU.max)

        z2_pairs = new("z2_pairs", [P, 2, COLS, 2], BF16)
        for t in range(PACK):
            mb = new(f"mb{t}", [P, 2 * COLS], F32)
            for i in range(2):
                nc.scalar.activation(mb[:, i * COLS : (i + 1) * COLS], s[t][:].indirect(entries(n3_l, i * COLS, COLS)), COPY)
            mx = new(f"mx{t}", [P, COLS], F32, reuse="mx")
            nc.vector.tensor_tensor(mx[:], mb[:, 0 : 2 * COLS : 2], mb[:, 1 : 2 * COLS : 2], ALU.max)
            st = new(f"st{t}", [P, COLS], F32)
            nc.vector.scalar_tensor_tensor(st[:], s_acc[t][:], S_FACTOR, mx[:], ALU.mult, ALU.subtract)
            st_n4 = new(f"st_n4_{t}", [P, COLS], F32)
            for i, cols in enumerate(halves):
                nc.vector.tensor_copy(st_n4[:, cols], st[:].indirect(entries(n4_l, i * HALF, HALF)))
            larger = new(f"larger{t}", [P, COLS], F32)
            nc.vector.tensor_tensor(larger[:], st[:], st_n4[:], ALU.max)
            nc.vector.tensor_scalar(z2_pairs[:, t // 2, :, t % 2], larger[:], gk_t[:, t : t + 1], None, ALU.mult)

        w3_codes = deal_fp4_words("w3_codes", w3_raw, slice(0, PACK), nc.gpsimd, reuse="key_picked")
        w3_scales_dealt = deal_scale_bytes("w3_scales_dealt", w3_scale_raw, nc.gpsimd, reuse="w3_raw")
        w2_scales_dealt = deal_scale_bytes("w2_scales_dealt", w2_scale_raw, nc.gpsimd, reuse="larger0")
        w2_codes = deal_fp4_words("w2_codes_low", w2_raw, slice(0, 2), nc.gpsimd, reuse="larger1")
        w2_codes = w2_codes + deal_fp4_words("w2_codes_high", w2_raw, slice(2, PACK), nc.gpsimd, reuse="larger2")
        z2_codes, z2_scales = quantise("z2", z2_pairs, [whole])

        z_pairs = new("z_pairs", [P, 2, COLS, 2], BF16, reuse="z2_pairs")
        for t in range(PACK):
            dt = new(f"dt{t}", [P, COLS], F32, reuse=f"s{t}" if t > 1 else None)
            nc.scalar.activation(dt[:].indirect(n1_l[:]), ra[:, t, :], COPY)
            nc.scalar.activation(dt[:].indirect(n2_l[:]), rb[:, t, :], COPY)
            for cols in halves if t == LAST else [whole]:
                nc.vector.tensor_scalar(z_pairs[:, t // 2, cols, t % 2], dt[:, cols], gn_t[:, t : t + 1], None, ALU.mult)
        z_codes, z_scales = quantise("z", z_pairs, halves)

        h_first = [psum.tile([P, COLS], F32, name="h_first_" + bank, tag=bank) for bank in ("bank_a0", "bank_b0")]
        h_acc = {t: psum.tile([P, COLS], F32, name=f"h_acc{t}", tag=f"bank_a{t}") for t in range(1, PACK)}
        for acc, cols in zip(h_first, halves):
            fp4_product(acc[:, cols], w3_codes, w3_scales_dealt, 0, z2_codes[:, cols], z2_scales[:, cols], True, False)
        for t in range(1, PACK):
            fp4_product(h_acc[t][:], w3_codes, w3_scales_dealt, t, z2_codes[:], z2_scales[:], True, False)
        for acc, cols in zip(h_first, halves):
            fp4_product(acc[:, cols], w2_codes, w2_scales_dealt, 0, z_codes[:, cols], z_scales[:, cols], False, True)
        for t in range(1, PACK):
            fp4_product(h_acc[t][:], w2_codes, w2_scales_dealt, t, z_codes[:], z_scales[:], False, True)

        result = new("result", [P, PACK, COLS], F32)
        rounded = new("rounded", [P, COLS, PACK], BF16)
        out_rows = out_0.rearrange("(p t) c -> p t c", t=PACK)
        h, st2 = [], []

        def copy_h(t):
            h_t = new(f"h{t}", [P, COLS], F32)
            if t == 0:
                for acc, cols in zip(h_first, halves):
                    nc.vector.tensor_copy(h_t[:, cols], acc[:, cols])
            else:
                nc.vector.tensor_copy(h_t[:], h_acc[t][:])
            h.append(h_t)

        def gated(t, engine, h_source):
            gate = new(f"gate{t}", [P, COLS], F32)
            for i, cols in enumerate(halves):
                nc.scalar.activation(gate[:, cols], h[t][:].indirect(entries(n5_l, i * HALF, HALF)), SIGMOID)
            st2_t = new(f"st2_{t}", [P, COLS], F32)
            engine.tensor_tensor(st2_t[:], h_source[:], gate[:], ALU.mult)
            st2.append(st2_t)

        def fetch_n6(t, fetch):
            fetched = new(f"st2_n6_{t}", [P, COLS], F32)
            for i, cols in enumerate(halves):
                fetch(fetched[:, cols], st2[t][:].indirect(entries(n6_l, i * HALF, HALF)))
            return fetched

        def scalar_fetch(dst, looked_up):
            nc.scalar.activation(dst, looked_up, COPY)

        def subtract(engine, t, spans, fetched):
            for cols in spans:
                engine.tensor_tensor(result[:, t, cols], st2[t][:, cols], fetched[:, cols], ALU.subtract)

        def finish_early(t):
            subtract(nc.gpsimd, t, halves, fetch_n6(t, nc.vector.tensor_copy))
            nc.sync.dma_start(out_rows[:, t, :], result[:, t, :])

        for t in range(LAST):
            copy_h(t)
        out_codes = new("out_codes", [P, COLS], U32)
        out_scales = new("out_scales", [P, COLS], U8)
        out_words = out_1[0].rearrange("p n t -> p (n t)").bitcast(I32)

        gated(0, nc.vector, h[0])
        copy_h(LAST)
        finish_early(0)
        gated(1, nc.gpsimd, h[1])
        gated(2, nc.vector, h_acc[2])
        finish_early(1)
        gated(LAST, nc.vector, h_acc[LAST])
        subtract(nc.vector, 2, [whole], fetch_n6(2, scalar_fetch))
        subtract(nc.vector, LAST, halves, fetch_n6(LAST, scalar_fetch))
        nc.sync.dma_start(out_rows[:, 2:, :], result[:, 2:, :])

        for cols, copy in zip(halves, (nc.scalar.copy, nc.vector.tensor_copy)):
            copy(
                rounded[:, cols, :].rearrange("p (c i) t -> p c t i", i=4),
                result[:, :, cols].rearrange("p t (c i) -> p c t i", i=4),
            )
        for cols in reversed(halves):
            nc.vector.quantize_mx(
                out_codes[:, cols].bitcast(FP8X4), out_scales[:, cols], rounded[:, cols, :].rearrange("p c t -> p (c t)")
            )
            nc.sync.dma_start(out_words[:, cols], out_codes[:, cols].bitcast(I32))
        for q in range(QUADS):
            nc.sync.dma_start(
                out_2[0, SCALE_ROWS * q : SCALE_ROWS * (q + 1), :].bitcast(I32),
                out_scales[QUAD * q : QUAD * q + SCALE_ROWS, :].bitcast(I32),
            )
